import numpy as np
import ml_dtypes


def mxq(x, axis, fmt="e4m3"):
    dtype, down = {"e4m3": (ml_dtypes.float8_e4m3fn, 7), "e5m2": (ml_dtypes.float8_e5m2, 14)}[fmt]
    v = np.moveaxis(np.asarray(x, np.float32).astype(ml_dtypes.bfloat16).astype(np.float64), axis, -1)
    blocks = v.reshape(v.shape[:-1] + (-1, 32))
    amax = np.abs(blocks).max(-1, keepdims=True)
    byte = np.maximum(np.where(amax > 0, np.frexp(amax)[1] - 1 + 127, 0) - down, 1)
    scale = np.exp2(byte - 127.0)
    codes = (blocks / scale).astype(np.float32).astype(dtype).astype(np.float64)
    return np.moveaxis((codes * scale).reshape(v.shape), -1, axis)


WIDE = False


def mx_kscale(k):
    if not WIDE:
        return np.ones(k)
    levels = np.array([24, -24, 12, -12, 0])
    if k % 512:
        return np.exp2(np.random.permutation(np.resize(levels, k // 32))).repeat(32)
    a = np.empty((k // 512, 16))
    for p in range(k // 512):
        a[p, :8] = np.random.permutation(np.resize(levels, 8))
        for g in range(8):
            far = levels[np.abs(levels - a[p, g]) >= 10]
            a[p, g + 8] = far[np.random.randint(len(far))]
    return np.exp2(a.ravel()).repeat(32)


def f64(x):
    return np.asarray(x).astype(np.float64)


def striped(idx):
    return np.tile(idx.reshape(-1, 16).T, (8, 1)).astype(np.uint16)


def unstriped(offs):
    return offs[:16].T.reshape(-1).astype(np.int64)


E2M1 = np.array([0.0, 0.5, 1.0, 1.5, 2.0, 3.0, 4.0, 6.0, -0.0, -0.5, -1.0, -1.5, -2.0, -3.0, -4.0, -6.0])


def pack_weight(w, fmt):
    k, n = w.shape
    w = f64(np.asarray(w, np.float32).astype(ml_dtypes.bfloat16)).reshape(k // 32, 32, n)
    amax = np.abs(w).max(1)
    if fmt == "e4m3":
        byte = np.frexp(amax)[1] - 1 + 127 - 7
    else:
        mant, ex = np.frexp(amax / 6.0)
        byte = np.where(mant > 0.5, ex, ex - 1) + 127
    byte = np.clip(np.where(amax > 0, byte, 1), 1, 254)
    scaled = (w * np.exp2(127.0 - byte)[:, None, :]).reshape(k, n).astype(np.float32)
    by_word = np.ascontiguousarray(scaled.reshape(k // 512, 128, 4, n).transpose(0, 1, 3, 2))
    if fmt == "e4m3":
        words = by_word.astype(ml_dtypes.float8_e4m3fn).view(np.uint8)
    else:
        c = by_word.astype(ml_dtypes.float4_e2m1fn).view(np.uint8) & 0xF
        words = (c[..., 0::2] | (c[..., 1::2] << 4)).reshape(k // 512, 128, 2 * n)
    return np.ascontiguousarray(words), np.ascontiguousarray(byte.astype(np.uint8).reshape(k // 512, 16, n))


def unpack_weight(words, scales, fmt):
    g, _, n = scales.shape
    words = np.ascontiguousarray(words).reshape(g, 128, n, -1)
    if fmt == "e4m3":
        vals = words.view(ml_dtypes.float8_e4m3fn).astype(np.float64)
    else:
        nib = np.empty((g, 128, n, 4), np.uint8)
        nib[..., 0::2] = words & 0xF
        nib[..., 1::2] = words >> 4
        vals = E2M1[nib]
    vals = vals * np.repeat(np.exp2(scales.astype(np.float64) - 127.0), 8, axis=1)[..., None]
    return vals.transpose(0, 1, 3, 2).reshape(g * 512, n)


def pack_table4(v):
    words, scales = pack_weight(v, "e2m1")
    g, t = words.shape[0] // 2, v.shape[1]
    return np.ascontiguousarray(words.reshape(g, 2, 128, t, 2).transpose(0, 2, 3, 1, 4).reshape(g, 128, t, 4)), scales


def unpack_table4(words, scales):
    g, _, t, _ = words.shape
    return unpack_weight(words.reshape(g, 128, t, 2, 2).transpose(0, 3, 1, 2, 4).reshape(2 * g, 128, 2 * t), scales, "e2m1")


def sigm(f):
    return 1.0 / (1.0 + np.exp(-np.maximum(f, -700.0)))


K, N, T, J = 1024, 1024, 2048, 1024


def setup_inputs():
    n = np.random.standard_normal
    s = mx_kscale(K)[:, None]
    p_tab = pack_table4(n((K, T)) * s)
    p_wk = pack_weight(n((K, N)) / np.sqrt(K) / s, "e2m1")
    p_wv4 = pack_weight(n((K, N)) / np.sqrt(K) / s, "e2m1")
    return {
        "tab_words": p_tab[0],
        "tab_scales": p_tab[1],
        "wk_words": p_wk[0],
        "wk_scales": p_wk[1],
        "wv4_words": p_wv4[0],
        "wv4_scales": p_wv4[1],
        "wvd": (0.4 * (n((K, N)) / np.sqrt(K) / s)).astype(np.float32),
        "st": (n((N, J))).astype(np.float32),
        "res": (n((N, J))).astype(np.float32),
        "offs": striped(np.random.permutation(T)[:J]),
    }


def reference(tab_words, tab_scales, wk_words, wk_scales, wv4_words, wv4_scales, wvd, st, res, offs):
    idx = unstriped(offs)
    tab_ = unpack_table4(tab_words, tab_scales)[:, idx]
    wk_ = unpack_weight(wk_words, wk_scales, "e2m1")
    wv4_ = unpack_weight(wv4_words, wv4_scales, "e2m1")
    wvd_ = mxq(f64(wvd), 0, "e4m3")
    ke = wk_.T @ tab_
    ve = wv4_.T @ tab_ + wvd_.T @ tab_
    gate = sigm(ke + f64(st))
    return f64(res) + gate * ve

@@ -1,0 +1,190 @@
+from contextlib import ExitStack
+
+import concourse.mybir as mybir
+
+K, N, T, J = 1024, 1024, 2048, 1024
+FLOPS = 3 * 2 * K * N * J
+
+F32 = mybir.dt.float32
+BF16 = mybir.dt.bfloat16
+I32 = mybir.dt.int32
+U32 = mybir.dt.uint32
+U16 = mybir.dt.uint16
+U8 = mybir.dt.uint8
+FP8X4 = mybir.dt.float8_e4m3fn_x4
+FP4X4 = mybir.dt.float4_e2m1fn_x4
+ADD = mybir.AluOpType.add
+MULT = mybir.AluOpType.mult
+SIGMOID = mybir.ActivationFunctionType.Sigmoid
+
+P = 128
+PASSES = 2
+JH = 512
+GROUP = 256
+N_TILES = N // P
+
+
+def tile_list_engram_dl_add_kernel(
+    tc, tab_words, tab_scales, wk_words, wk_scales, wv4_words, wv4_scales, wvd, st, res, offs, out
+):
+    nc = tc.nc
+    with ExitStack() as ctx:
+        keep = ctx.enter_context(tc.tile_pool(name="keep", bufs=1))
+        psum = ctx.enter_context(tc.psum_pool(name="psum", bufs=4))
+
+        offsets = keep.tile([P, J // 16], U16, name="offsets")
+        tab_sc = keep.tile([P, PASSES, T], U8, name="tab_sc", align_bytes=64)
+        wk_sc = keep.tile([P, PASSES, N], U8, name="wk_sc", align_bytes=64)
+        wv_sc = keep.tile([P, PASSES, N], U8, name="wv_sc", align_bytes=64)
+        tab_w = keep.tile([P, T], I32, name="tab_w", align_bytes=64)
+        warm = keep.tile([P, 2], F32, name="warm")
+
+        nc.vector.memset(tab_sc[:].bitcast(I32), 0)
+        nc.gpsimd.memset(wk_sc[:].bitcast(I32), 0)
+        nc.vector.memset(wv_sc[:].bitcast(I32), 0)
+        nc.vector.memset(warm[:], 0.0)
+        nc.scalar.activation(warm[:, 1:2], warm[:, 0:1], SIGMOID)
+
+        def load_scales(queue, plane, dram):
+            rows = dram.rearrange("a (q r) n -> r q a n", r=4)
+            for r in range(4):
+                queue.dma_start(plane[r:P:32, :, :].bitcast(I32), rows[r].bitcast(I32))
+
+        def load_words(name, dram, half):
+            words = keep.tile([P, PASSES, N], U8, name=name, align_bytes=64)
+            src = dram[:, :, half * N : (half + 1) * N].rearrange("a p b -> p a b")
+            nc.sync.dma_start(words[:].bitcast(I32), src.bitcast(I32))
+            return words
+
+        def load_wvd(a, c0, c1):
+            raw = keep.tile([P, 4, c1 - c0], F32, name="wvd_raw_%d_%d" % (a, c0), align_bytes=64)
+            src = wvd[512 * a : 512 * (a + 1), c0:c1].rearrange("(p t) n -> p t n", t=4)
+            nc.sync.dma_start(raw[:], src)
+            for g in range(c0 // GROUP, c1 // GROUP):
+                wvd_raw[a, g] = raw[:, :, g * GROUP - c0 : (g + 1) * GROUP - c0]
+
+        def load_rows(name, dram, pair):
+            rows = keep.tile([P, 2, J], F32, name="%s_%d" % (name, pair), align_bytes=64)
+            nc.sync.dma_start(rows[:], dram[2 * P * pair : 2 * P * (pair + 1), :].rearrange("(i p) j -> p i j", p=P))
+            return rows
+
+        wvd_raw, st_sb, res_sb, wk_w, wv_w = {}, {}, {}, {}, {}
+        nc.sync.dma_start(offsets[:], offs)
+        load_scales(nc.sync, tab_sc, tab_scales)
+        load_scales(nc.gpsimd, wk_sc, wk_scales)
+        nc.sync.dma_start(tab_w[:], tab_words[0].rearrange("p t b -> p (t b)").bitcast(I32))
+        load_wvd(0, 0, 256)
+        load_wvd(1, 0, 256)
+        wk_w[0] = load_words("wk_w0", wk_words, 0)
+        wv_w[0] = load_words("wv_w0", wv4_words, 0)
+        load_scales(nc.sync, wv_sc, wv4_scales)
+        st_sb[0] = load_rows("st", st, 0)
+        load_wvd(0, 256, 512)
+        load_wvd(1, 256, 512)
+        st_sb[1] = load_rows("st", st, 1)
+        load_wvd(0, 512, 1024)
+        wk_w[1] = load_words("wk_w1", wk_words, 1)
+        wv_w[1] = load_words("wv_w1", wv4_words, 1)
+        load_wvd(1, 512, 1024)
+        st_sb[2] = load_rows("st", st, 2)
+        res_sb[0] = load_rows("res", res, 0)
+        st_sb[3] = load_rows("st", st, 3)
+        for pair in range(1, 4):
+            res_sb[pair] = load_rows("res", res, pair)
+
+        v_w, v_sc = {}, {}
+
+        def gather(h):
+            picks = offsets[:, h * (JH // 16) : (h + 1) * (JH // 16)]
+            for a in range(PASSES):
+                sc = keep.tile([P, JH], U8, name="v_sc_%d_%d" % (h, a), align_bytes=64)
+                nc.vector.tensor_copy(sc[:], tab_sc[:, a, :].indirect(picks))
+                v_sc[h, a] = sc
+            both = keep.tile([P, JH], U32, name="v_both_%d" % h, align_bytes=64)
+            nc.vector.tensor_copy(both[:], tab_w[:].bitcast(U32).indirect(picks))
+            halves = both[:].bitcast(U16).rearrange("p (j d) -> p d j", d=2)
+            for a in range(PASSES):
+                w = keep.tile([P, 2 * JH], U8, name="v_w_%d_%d" % (h, a), align_bytes=64)
+                nc.vector.tensor_copy(w[:].bitcast(U16), halves[:, a, :])
+                v_w[h, a] = w
+
+        wd_codes, wd_sc = {}, {}
+
+        def quantise(g):
+            for a in range(PASSES):
+                grouped = keep.tile([P, GROUP * 4], BF16, name="grouped_%d_%d" % (g, a), align_bytes=64)
+                nc.scalar.copy(
+                    grouped[:].rearrange("p (c i t) -> p c t i", i=4, t=4),
+                    wvd_raw[a, g].rearrange("p t (c i) -> p c t i", i=4),
+                )
+                codes = keep.tile([P, GROUP], U32, name="wd_codes_%d_%d" % (g, a), align_bytes=64)
+                sc = keep.tile([P, GROUP], U8, name="wd_sc_%d_%d" % (g, a), align_bytes=64)
+                nc.vector.quantize_mx(codes[:].bitcast(FP8X4), sc[:], grouped[:])
+                wd_codes[g, a], wd_sc[g, a] = codes, sc
+
+        def fp4_passes(acc, words, plane, i, h, last):
+            c = (i % 4) * P
+            for a in range(PASSES):
+                nc.tensor.matmul_mx(
+                    acc[:],
+                    lhsT=words[i // 4][:, a, 2 * c : 2 * (c + P)].bitcast(FP4X4),
+                    lhsT_scale=plane[:, a, i * P : (i + 1) * P],
+                    rhs=v_w[h, a][:].bitcast(FP4X4),
+                    rhs_scale=v_sc[h, a][:],
+                    start=(a == 0),
+                    stop=(last and a == PASSES - 1),
+                )
+
+        def fp8_passes(acc, i, h):
+            c = (i % 2) * P
+            for a in range(PASSES):
+                nc.tensor.matmul_mx(
+                    acc[:],
+                    lhsT=wd_codes[i // 2, a][:, c : c + P].bitcast(FP8X4),
+                    lhsT_scale=wd_sc[i // 2, a][:, c : c + P],
+                    rhs=v_w[h, a][:].bitcast(FP4X4),
+                    rhs_scale=v_sc[h, a][:],
+                    start=False,
+                    stop=(a == PASSES - 1),
+                )
+
+        def unit(i, h):
+            cols = slice(h * JH, (h + 1) * JH)
+            gate = st_sb[i // 2][:, i % 2, cols]
+            acc = res_sb[i // 2][:, i % 2, cols]
+            ke = psum.tile([P, JH], F32, name="ke")
+            fp4_passes(ke, wk_w, wk_sc, i, h, True)
+            ve = psum.tile([P, JH], F32, name="ve")
+            fp4_passes(ve, wv_w, wv_sc, i, h, False)
+            fp8_passes(ve, i, h)
+            nc.vector.tensor_tensor(gate, ke[:], gate, ADD)
+            nc.scalar.activation(gate, gate, SIGMOID)
+            nc.vector.tensor_tensor(gate, ve[:], gate, MULT)
+            adder = nc.gpsimd if i < 6 else nc.vector
+            adder.tensor_tensor(acc, acc, gate, ADD)
+
+        def store(i):
+            rows = out[i * P : (i + 1) * P, :]
+            if i < N_TILES - 1:
+                nc.sync.dma_start(rows, res_sb[i // 2][:, i % 2, :])
+            else:
+                for h in range(2):
+                    cols = slice(h * JH, (h + 1) * JH)
+                    nc.sync.dma_start(rows[:, cols], res_sb[i // 2][:, i % 2, cols])
+
+        gather(0)
+        quantise(0)
+        gather(1)
+        unit(0, 0)
+        unit(1, 0)
+        quantise(1)
+        unit(0, 1)
+        store(0)
+        unit(1, 1)
+        store(1)
+        for i in range(2, N_TILES):
+            if i % 2 == 0 and i // 2 + 1 < N // GROUP:
+                quantise(i // 2 + 1)
+            unit(i, 0)
+            unit(i, 1)
+            store(i)

@@ -39,8 +39,8 @@ def tile_list_engram_dl_add_kernel(
         tab_w = keep.tile([P, T], I32, name="tab_w", align_bytes=64)
         warm = keep.tile([P, 2], F32, name="warm")
 
-        nc.vector.memset(tab_sc[:].bitcast(I32), 0)
-        nc.gpsimd.memset(wk_sc[:].bitcast(I32), 0)
+        nc.gpsimd.memset(tab_sc[:].bitcast(I32), 0)
+        nc.vector.memset(wk_sc[:].bitcast(I32), 0)
         nc.vector.memset(wv_sc[:].bitcast(I32), 0)
         nc.vector.memset(warm[:], 0.0)
         nc.scalar.activation(warm[:, 1:2], warm[:, 0:1], SIGMOID)
@@ -50,10 +50,9 @@ def tile_list_engram_dl_add_kernel(
             for r in range(4):
                 queue.dma_start(plane[r:P:32, :, :].bitcast(I32), rows[r].bitcast(I32))
 
-        def load_words(name, dram, half):
-            words = keep.tile([P, PASSES, N], U8, name=name, align_bytes=64)
-            src = dram[:, :, half * N : (half + 1) * N].rearrange("a p b -> p a b")
-            nc.sync.dma_start(words[:].bitcast(I32), src.bitcast(I32))
+        def load_words(name, dram):
+            words = keep.tile([P, PASSES, 2 * N], U8, name=name, align_bytes=64)
+            nc.sync.dma_start(words[:].bitcast(I32), dram.rearrange("a p b -> p a b").bitcast(I32))
             return words
 
         def load_wvd(a, c0, c1):
@@ -63,50 +62,70 @@ def tile_list_engram_dl_add_kernel(
             for g in range(c0 // GROUP, c1 // GROUP):
                 wvd_raw[a, g] = raw[:, :, g * GROUP - c0 : (g + 1) * GROUP - c0]
 
-        def load_rows(name, dram, pair):
-            rows = keep.tile([P, 2, J], F32, name="%s_%d" % (name, pair), align_bytes=64)
-            nc.sync.dma_start(rows[:], dram[2 * P * pair : 2 * P * (pair + 1), :].rearrange("(i p) j -> p i j", p=P))
+        def load_rows(name, dram, i):
+            rows = keep.tile([P, J], F32, name="%s_%d" % (name, i), align_bytes=64)
+            nc.sync.dma_start(rows[:], dram[P * i : P * (i + 1), :])
             return rows
 
-        wvd_raw, st_sb, res_sb, wk_w, wv_w = {}, {}, {}, {}, {}
+        wvd_raw, st_sb, res_sb = {}, {}, {}
         nc.sync.dma_start(offsets[:], offs)
-        load_scales(nc.sync, tab_sc, tab_scales)
-        load_scales(nc.gpsimd, wk_sc, wk_scales)
+        load_scales(nc.gpsimd, tab_sc, tab_scales)
         nc.sync.dma_start(tab_w[:], tab_words[0].rearrange("p t b -> p (t b)").bitcast(I32))
-        load_wvd(0, 0, 256)
-        load_wvd(1, 0, 256)
-        wk_w[0] = load_words("wk_w0", wk_words, 0)
-        wv_w[0] = load_words("wv_w0", wv4_words, 0)
+        load_scales(nc.sync, wk_sc, wk_scales)
+        wk_w = load_words("wk_w", wk_words)
+        load_wvd(0, 0, 512)
         load_scales(nc.sync, wv_sc, wv4_scales)
+        wv_w = load_words("wv_w", wv4_words)
+        load_wvd(1, 0, 256)
         st_sb[0] = load_rows("st", st, 0)
-        load_wvd(0, 256, 512)
         load_wvd(1, 256, 512)
         st_sb[1] = load_rows("st", st, 1)
-        load_wvd(0, 512, 1024)
-        wk_w[1] = load_words("wk_w1", wk_words, 1)
-        wv_w[1] = load_words("wv_w1", wv4_words, 1)
-        load_wvd(1, 512, 1024)
         st_sb[2] = load_rows("st", st, 2)
-        res_sb[0] = load_rows("res", res, 0)
+        load_wvd(0, 512, 1024)
         st_sb[3] = load_rows("st", st, 3)
-        for pair in range(1, 4):
-            res_sb[pair] = load_rows("res", res, pair)
+        load_wvd(1, 512, 1024)
+        st_sb[4] = load_rows("st", st, 4)
+        res_sb[0] = load_rows("res", res, 0)
+        res_sb[1] = load_rows("res", res, 1)
+        st_sb[5] = load_rows("st", st, 5)
+        res_sb[2] = load_rows("res", res, 2)
+        st_sb[6] = load_rows("st", st, 6)
+        res_sb[3] = load_rows("res", res, 3)
+        res_sb[4] = load_rows("res", res, 4)
+        st_sb[7] = load_rows("st", st, 7)
+        res_sb[5] = load_rows("res", res, 5)
+        res_sb[6] = load_rows("res", res, 6)
+        res_sb[7] = load_rows("res", res, 7)
 
         v_w, v_sc = {}, {}
 
         def gather(h):
             picks = offsets[:, h * (JH // 16) : (h + 1) * (JH // 16)]
-            for a in range(PASSES):
-                sc = keep.tile([P, JH], U8, name="v_sc_%d_%d" % (h, a), align_bytes=64)
-                nc.vector.tensor_copy(sc[:], tab_sc[:, a, :].indirect(picks))
-                v_sc[h, a] = sc
-            both = keep.tile([P, JH], U32, name="v_both_%d" % h, align_bytes=64)
-            nc.vector.tensor_copy(both[:], tab_w[:].bitcast(U32).indirect(picks))
-            halves = both[:].bitcast(U16).rearrange("p (j d) -> p d j", d=2)
-            for a in range(PASSES):
+            if h == 0:
+                picked = keep.tile([P, 4 * JH], U8, name="picked0", tag="picked", align_bytes=64)
+                planes = keep.tile([P, PASSES * JH], U8, name="planes0", align_bytes=64)[:]
+            else:
+                picked = keep.tile([P, 6 * JH], U8, name="picked1", tag="picked", align_bytes=64)
+                planes = picked[:, 4 * JH :]
+            both = picked[:, : 4 * JH]
+
+            def scales(a):
+                v_sc[h, a] = planes[:, a * JH : (a + 1) * JH]
+                nc.vector.tensor_copy(v_sc[h, a], tab_sc[:, a, :].indirect(picks))
+
+            def words():
+                nc.vector.tensor_copy(both.bitcast(U32), tab_w[:].bitcast(U32).indirect(picks))
+
+            def part(a):
+                halves = both.bitcast(U16).rearrange("p (j d) -> p d j", d=2)
                 w = keep.tile([P, 2 * JH], U8, name="v_w_%d_%d" % (h, a), align_bytes=64)
                 nc.vector.tensor_copy(w[:].bitcast(U16), halves[:, a, :])
                 v_w[h, a] = w
+
+            if h == 0:
+                words(); part(0); part(1); scales(0); scales(1)
+            else:
+                words(); scales(0); part(0); part(1); scales(1)
 
         wd_codes, wd_sc = {}, {}
 
@@ -123,14 +142,14 @@ def tile_list_engram_dl_add_kernel(
                 wd_codes[g, a], wd_sc[g, a] = codes, sc
 
         def fp4_passes(acc, words, plane, i, h, last):
-            c = (i % 4) * P
+            c = i * P
             for a in range(PASSES):
                 nc.tensor.matmul_mx(
                     acc[:],
-                    lhsT=words[i // 4][:, a, 2 * c : 2 * (c + P)].bitcast(FP4X4),
+                    lhsT=words[:, a, 2 * c : 2 * (c + P)].bitcast(FP4X4),
                     lhsT_scale=plane[:, a, i * P : (i + 1) * P],
                     rhs=v_w[h, a][:].bitcast(FP4X4),
-                    rhs_scale=v_sc[h, a][:],
+                    rhs_scale=v_sc[h, a],
                     start=(a == 0),
                     stop=(last and a == PASSES - 1),
                 )
@@ -143,34 +162,38 @@ def tile_list_engram_dl_add_kernel(
                     lhsT=wd_codes[i // 2, a][:, c : c + P].bitcast(FP8X4),
                     lhsT_scale=wd_sc[i // 2, a][:, c : c + P],
                     rhs=v_w[h, a][:].bitcast(FP4X4),
-                    rhs_scale=v_sc[h, a][:],
+                    rhs_scale=v_sc[h, a],
                     start=False,
                     stop=(a == PASSES - 1),
                 )
 
         def unit(i, h):
             cols = slice(h * JH, (h + 1) * JH)
-            gate = st_sb[i // 2][:, i % 2, cols]
-            acc = res_sb[i // 2][:, i % 2, cols]
+            gate = st_sb[i][:, cols]
             ke = psum.tile([P, JH], F32, name="ke")
             fp4_passes(ke, wk_w, wk_sc, i, h, True)
             ve = psum.tile([P, JH], F32, name="ve")
             fp4_passes(ve, wv_w, wv_sc, i, h, False)
             fp8_passes(ve, i, h)
-            nc.vector.tensor_tensor(gate, ke[:], gate, ADD)
+            nc.vector.tensor_tensor(gate, gate, ke[:], ADD)
             nc.scalar.activation(gate, gate, SIGMOID)
-            nc.vector.tensor_tensor(gate, ve[:], gate, MULT)
-            adder = nc.gpsimd if i < 6 else nc.vector
-            adder.tensor_tensor(acc, acc, gate, ADD)
+            nc.vector.tensor_tensor(gate, gate, ve[:], MULT)
+            if i < N_TILES - 1:
+                add_res(i, h)
+
+        def add_res(i, h):
+            cols = slice(h * JH, (h + 1) * JH)
+            adder = nc.gpsimd if i < 7 else nc.vector
+            adder.tensor_tensor(res_sb[i][:, cols], res_sb[i][:, cols], st_sb[i][:, cols], ADD)
 
         def store(i):
             rows = out[i * P : (i + 1) * P, :]
             if i < N_TILES - 1:
-                nc.sync.dma_start(rows, res_sb[i // 2][:, i % 2, :])
+                nc.sync.dma_start(rows, res_sb[i][:])
             else:
                 for h in range(2):
                     cols = slice(h * JH, (h + 1) * JH)
-                    nc.sync.dma_start(rows[:, cols], res_sb[i // 2][:, i % 2, cols])
+                    nc.sync.dma_start(rows[:, cols], res_sb[i][:, cols])
 
         gather(0)
         quantise(0)
@@ -187,4 +210,7 @@ def tile_list_engram_dl_add_kernel(
                 quantise(i // 2 + 1)
             unit(i, 0)
             unit(i, 1)
+            if i == N_TILES - 1:
+                add_res(i, 0)
+                add_res(i, 1)
             store(i)

@@ -39,9 +39,9 @@ def tile_list_engram_dl_add_kernel(
         tab_w = keep.tile([P, T], I32, name="tab_w", align_bytes=64)
         warm = keep.tile([P, 2], F32, name="warm")
 
-        nc.gpsimd.memset(tab_sc[:].bitcast(I32), 0)
+        nc.vector.memset(tab_sc[:].bitcast(I32), 0)
         nc.vector.memset(wk_sc[:].bitcast(I32), 0)
-        nc.vector.memset(wv_sc[:].bitcast(I32), 0)
+        nc.gpsimd.memset(wv_sc[:].bitcast(I32), 0)
         nc.vector.memset(warm[:], 0.0)
         nc.scalar.activation(warm[:, 1:2], warm[:, 0:1], SIGMOID)
 
@@ -69,30 +69,31 @@ def tile_list_engram_dl_add_kernel(
 
         wvd_raw, st_sb, res_sb = {}, {}, {}
         nc.sync.dma_start(offsets[:], offs)
-        load_scales(nc.gpsimd, tab_sc, tab_scales)
-        nc.sync.dma_start(tab_w[:], tab_words[0].rearrange("p t b -> p (t b)").bitcast(I32))
-        load_scales(nc.sync, wk_sc, wk_scales)
         wk_w = load_words("wk_w", wk_words)
-        load_wvd(0, 0, 512)
-        load_scales(nc.sync, wv_sc, wv4_scales)
+        load_scales(nc.sync, tab_sc, tab_scales)
+        load_scales(nc.gpsimd, wv_sc, wv4_scales)
+        nc.sync.dma_start(tab_w[:], tab_words[0].rearrange("p t b -> p (t b)").bitcast(I32))
+        load_wvd(0, 0, 256)
+        load_scales(nc.sync, wk_sc, wk_scales)
         wv_w = load_words("wv_w", wv4_words)
         load_wvd(1, 0, 256)
         st_sb[0] = load_rows("st", st, 0)
-        load_wvd(1, 256, 512)
         st_sb[1] = load_rows("st", st, 1)
+        load_wvd(0, 256, 512)
+        load_wvd(1, 256, 512)
         st_sb[2] = load_rows("st", st, 2)
+        res_sb[0] = load_rows("res", res, 0)
         load_wvd(0, 512, 1024)
         st_sb[3] = load_rows("st", st, 3)
         load_wvd(1, 512, 1024)
         st_sb[4] = load_rows("st", st, 4)
-        res_sb[0] = load_rows("res", res, 0)
         res_sb[1] = load_rows("res", res, 1)
         st_sb[5] = load_rows("st", st, 5)
         res_sb[2] = load_rows("res", res, 2)
         st_sb[6] = load_rows("st", st, 6)
         res_sb[3] = load_rows("res", res, 3)
-        res_sb[4] = load_rows("res", res, 4)
         st_sb[7] = load_rows("st", st, 7)
+        res_sb[4] = load_rows("res", res, 4)
         res_sb[5] = load_rows("res", res, 5)
         res_sb[6] = load_rows("res", res, 6)
         res_sb[7] = load_rows("res", res, 7)
@@ -123,7 +124,7 @@ def tile_list_engram_dl_add_kernel(
                 v_w[h, a] = w
 
             if h == 0:
-                words(); part(0); part(1); scales(0); scales(1)
+                scales(0); scales(1); words(); part(0); part(1)
             else:
                 words(); scales(0); part(0); part(1); scales(1)
 
@@ -167,50 +168,38 @@ def tile_list_engram_dl_add_kernel(
                     stop=(a == PASSES - 1),
                 )
 
-        def unit(i, h):
-            cols = slice(h * JH, (h + 1) * JH)
-            gate = st_sb[i][:, cols]
+        def key(i, h):
+            gate = st_sb[i][:, h * JH : (h + 1) * JH]
             ke = psum.tile([P, JH], F32, name="ke")
             fp4_passes(ke, wk_w, wk_sc, i, h, True)
+            nc.vector.tensor_tensor(gate, gate, ke[:], ADD)
+            nc.scalar.activation(gate, gate, SIGMOID)
+
+        def value(i, h):
+            gate = st_sb[i][:, h * JH : (h + 1) * JH]
             ve = psum.tile([P, JH], F32, name="ve")
             fp4_passes(ve, wv_w, wv_sc, i, h, False)
             fp8_passes(ve, i, h)
-            nc.vector.tensor_tensor(gate, gate, ke[:], ADD)
-            nc.scalar.activation(gate, gate, SIGMOID)
             nc.vector.tensor_tensor(gate, gate, ve[:], MULT)
-            if i < N_TILES - 1:
-                add_res(i, h)
 
-        def add_res(i, h):
+        def finish(i, h):
             cols = slice(h * JH, (h + 1) * JH)
-            adder = nc.gpsimd if i < 7 else nc.vector
+            adder = nc.gpsimd if 2 * i + h < 14 else nc.vector
             adder.tensor_tensor(res_sb[i][:, cols], res_sb[i][:, cols], st_sb[i][:, cols], ADD)
+            if i == N_TILES - 1:
+                nc.sync.dma_start(out[i * P : (i + 1) * P, cols], res_sb[i][:, cols])
+            elif h == 1:
+                nc.sync.dma_start(out[i * P : (i + 1) * P, :], res_sb[i][:])
 
-        def store(i):
-            rows = out[i * P : (i + 1) * P, :]
-            if i < N_TILES - 1:
-                nc.sync.dma_start(rows, res_sb[i][:])
-            else:
-                for h in range(2):
-                    cols = slice(h * JH, (h + 1) * JH)
-                    nc.sync.dma_start(rows[:, cols], res_sb[i][:, cols])
-
+        units = [(0, 0), (1, 0), (0, 1), (1, 1)] + [(i, h) for i in range(2, N_TILES) for h in range(2)]
         gather(0)
         quantise(0)
         gather(1)
-        unit(0, 0)
-        unit(1, 0)
-        quantise(1)
-        unit(0, 1)
-        store(0)
-        unit(1, 1)
-        store(1)
-        for i in range(2, N_TILES):
-            if i % 2 == 0 and i // 2 + 1 < N // GROUP:
-                quantise(i // 2 + 1)
-            unit(i, 0)
-            unit(i, 1)
-            if i == N_TILES - 1:
-                add_res(i, 0)
-                add_res(i, 1)
-            store(i)
+        key(*units[0])
+        for u, (i, h) in enumerate(units):
+            if u % 4 == 2 and u // 4 + 1 < N // GROUP:
+                quantise(u // 4 + 1)
+            if u + 1 < len(units):
+                key(*units[u + 1])
+            value(i, h)
+            finish(i, h)

@@ -18,10 +18,16 @@ MULT = mybir.AluOpType.mult
 SIGMOID = mybir.ActivationFunctionType.Sigmoid
 
 P = 128
-PASSES = 2
-JH = 512
+PACK = 4
+K_PASS = P * PACK
+PASSES = K // K_PASS
+HALF = 512
 GROUP = 256
-N_TILES = N // P
+ROW_TILES = N // P
+LIST_ROWS = 16
+BANKS = 4
+KEYS_AHEAD = 2
+VECTOR_ADDS = ((ROW_TILES - 2, 1), (ROW_TILES - 1, 1))
 
 
 def tile_list_engram_dl_add_kernel(
@@ -30,20 +36,19 @@ def tile_list_engram_dl_add_kernel(
     nc = tc.nc
     with ExitStack() as ctx:
         keep = ctx.enter_context(tc.tile_pool(name="keep", bufs=1))
-        psum = ctx.enter_context(tc.psum_pool(name="psum", bufs=4))
+        psum = ctx.enter_context(tc.psum_pool(name="psum", bufs=BANKS))
 
-        offsets = keep.tile([P, J // 16], U16, name="offsets")
+        offsets = keep.tile([P, J // LIST_ROWS], U16, name="offsets")
         tab_sc = keep.tile([P, PASSES, T], U8, name="tab_sc", align_bytes=64)
         wk_sc = keep.tile([P, PASSES, N], U8, name="wk_sc", align_bytes=64)
         wv_sc = keep.tile([P, PASSES, N], U8, name="wv_sc", align_bytes=64)
         tab_w = keep.tile([P, T], I32, name="tab_w", align_bytes=64)
-        warm = keep.tile([P, 2], F32, name="warm")
 
         nc.vector.memset(tab_sc[:].bitcast(I32), 0)
         nc.vector.memset(wk_sc[:].bitcast(I32), 0)
         nc.gpsimd.memset(wv_sc[:].bitcast(I32), 0)
-        nc.vector.memset(warm[:], 0.0)
-        nc.scalar.activation(warm[:, 1:2], warm[:, 0:1], SIGMOID)
+
+        wvd_raw, st_sb, res_sb = {}, {}, {}
 
         def load_scales(queue, plane, dram):
             rows = dram.rearrange("a (q r) n -> r q a n", r=4)
@@ -56,150 +61,151 @@ def tile_list_engram_dl_add_kernel(
             return words
 
         def load_wvd(a, c0, c1):
-            raw = keep.tile([P, 4, c1 - c0], F32, name="wvd_raw_%d_%d" % (a, c0), align_bytes=64)
-            src = wvd[512 * a : 512 * (a + 1), c0:c1].rearrange("(p t) n -> p t n", t=4)
+            raw = keep.tile([P, PACK, c1 - c0], F32, name="wvd_raw_%d_%d" % (a, c0), align_bytes=64)
+            src = wvd[K_PASS * a : K_PASS * (a + 1), c0:c1].rearrange("(p t) n -> p t n", t=PACK)
             nc.sync.dma_start(raw[:], src)
             for g in range(c0 // GROUP, c1 // GROUP):
                 wvd_raw[a, g] = raw[:, :, g * GROUP - c0 : (g + 1) * GROUP - c0]
 
-        def load_rows(name, dram, i):
-            rows = keep.tile([P, J], F32, name="%s_%d" % (name, i), align_bytes=64)
-            nc.sync.dma_start(rows[:], dram[P * i : P * (i + 1), :])
-            return rows
+        def load_rows(name, dram, tiles, indices):
+            for i in indices:
+                tiles[i] = keep.tile([P, J], F32, name="%s_%d" % (name, i), align_bytes=64)
+                nc.sync.dma_start(tiles[i][:], dram[P * i : P * (i + 1), :])
 
-        wvd_raw, st_sb, res_sb = {}, {}, {}
         nc.sync.dma_start(offsets[:], offs)
         wk_w = load_words("wk_w", wk_words)
         load_scales(nc.sync, tab_sc, tab_scales)
         load_scales(nc.gpsimd, wv_sc, wv4_scales)
         nc.sync.dma_start(tab_w[:], tab_words[0].rearrange("p t b -> p (t b)").bitcast(I32))
-        load_wvd(0, 0, 256)
-        load_scales(nc.sync, wk_sc, wk_scales)
+        load_wvd(0, 0, GROUP)
         wv_w = load_words("wv_w", wv4_words)
-        load_wvd(1, 0, 256)
-        st_sb[0] = load_rows("st", st, 0)
-        st_sb[1] = load_rows("st", st, 1)
-        load_wvd(0, 256, 512)
-        load_wvd(1, 256, 512)
-        st_sb[2] = load_rows("st", st, 2)
-        res_sb[0] = load_rows("res", res, 0)
-        load_wvd(0, 512, 1024)
-        st_sb[3] = load_rows("st", st, 3)
-        load_wvd(1, 512, 1024)
-        st_sb[4] = load_rows("st", st, 4)
-        res_sb[1] = load_rows("res", res, 1)
-        st_sb[5] = load_rows("st", st, 5)
-        res_sb[2] = load_rows("res", res, 2)
-        st_sb[6] = load_rows("st", st, 6)
-        res_sb[3] = load_rows("res", res, 3)
-        st_sb[7] = load_rows("st", st, 7)
-        res_sb[4] = load_rows("res", res, 4)
-        res_sb[5] = load_rows("res", res, 5)
-        res_sb[6] = load_rows("res", res, 6)
-        res_sb[7] = load_rows("res", res, 7)
+        load_scales(nc.sync, wk_sc, wk_scales)
+        load_wvd(0, GROUP, 2 * GROUP)
+        load_rows("res", res, res_sb, [0])
+        load_wvd(1, 0, 2 * GROUP)
+        load_rows("st", st, st_sb, [0, 1])
+        load_wvd(0, 2 * GROUP, 3 * GROUP)
+        load_rows("st", st, st_sb, [2])
+        load_rows("res", res, res_sb, [1, 2])
+        load_wvd(0, 3 * GROUP, 4 * GROUP)
+        load_rows("st", st, st_sb, [3])
+        load_wvd(1, 2 * GROUP, 4 * GROUP)
+        load_rows("st", st, st_sb, [4, 5])
+        load_rows("res", res, res_sb, [3, 4, 5, 6])
+        load_rows("st", st, st_sb, [6, 7])
+        load_rows("res", res, res_sb, [7])
 
         v_w, v_sc = {}, {}
 
-        def gather(h):
-            picks = offsets[:, h * (JH // 16) : (h + 1) * (JH // 16)]
-            if h == 0:
-                picked = keep.tile([P, 4 * JH], U8, name="picked0", tag="picked", align_bytes=64)
-                planes = keep.tile([P, PASSES * JH], U8, name="planes0", align_bytes=64)[:]
-            else:
-                picked = keep.tile([P, 6 * JH], U8, name="picked1", tag="picked", align_bytes=64)
-                planes = picked[:, 4 * JH :]
-            both = picked[:, : 4 * JH]
+        def picks(h):
+            return offsets[:, h * (HALF // LIST_ROWS) : (h + 1) * (HALF // LIST_ROWS)]
 
-            def scales(a):
-                v_sc[h, a] = planes[:, a * JH : (a + 1) * JH]
-                nc.vector.tensor_copy(v_sc[h, a], tab_sc[:, a, :].indirect(picks))
+        def gather_scales(h, a, planes):
+            v_sc[h, a] = planes[:, a * HALF : (a + 1) * HALF]
+            nc.vector.tensor_copy(v_sc[h, a], tab_sc[:, a, :].indirect(picks(h)))
 
-            def words():
-                nc.vector.tensor_copy(both.bitcast(U32), tab_w[:].bitcast(U32).indirect(picks))
+        def gather_words(h, both):
+            nc.vector.tensor_copy(both.bitcast(U32), tab_w[:].bitcast(U32).indirect(picks(h)))
 
-            def part(a):
-                halves = both.bitcast(U16).rearrange("p (j d) -> p d j", d=2)
-                w = keep.tile([P, 2 * JH], U8, name="v_w_%d_%d" % (h, a), align_bytes=64)
-                nc.vector.tensor_copy(w[:].bitcast(U16), halves[:, a, :])
-                v_w[h, a] = w
+        def by_pass(h, both):
+            parted = keep.tile([P, PASSES, 2 * HALF], U8, name="v_w_%d" % h, align_bytes=64)
+            for a in range(PASSES):
+                v_w[h, a] = parted[:, a, :]
+            return parted[:].bitcast(U16), both.bitcast(U16).rearrange("p (j d) -> p d j", d=PASSES)
 
-            if h == 0:
-                scales(0); scales(1); words(); part(0); part(1)
-            else:
-                words(); scales(0); part(0); part(1); scales(1)
+        def gather_first_half():
+            both = keep.tile([P, 4 * HALF], U8, name="picked0", tag="picked", align_bytes=64)
+            planes = keep.tile([P, PASSES * HALF], U8, name="planes0", align_bytes=64)
+            parted, paired = by_pass(0, both[:])
+            for a in range(PASSES):
+                gather_scales(0, a, planes[:])
+            gather_words(0, both[:])
+            for a in range(PASSES):
+                nc.vector.tensor_copy(parted[:, a, :], paired[:, a, :])
+
+        def gather_second_half():
+            picked = keep.tile([P, 6 * HALF], U8, name="picked1", tag="picked", align_bytes=64)
+            both, planes = picked[:, : 4 * HALF], picked[:, 4 * HALF :]
+            parted, paired = by_pass(1, both)
+            gather_words(1, both)
+            gather_scales(1, 0, planes)
+            nc.vector.tensor_copy(parted, paired)
+            gather_scales(1, 1, planes)
 
         wd_codes, wd_sc = {}, {}
 
         def quantise(g):
             for a in range(PASSES):
-                grouped = keep.tile([P, GROUP * 4], BF16, name="grouped_%d_%d" % (g, a), align_bytes=64)
+                grouped = keep.tile([P, GROUP * PACK], BF16, name="grouped_%d_%d" % (g, a), align_bytes=64)
                 nc.scalar.copy(
-                    grouped[:].rearrange("p (c i t) -> p c t i", i=4, t=4),
+                    grouped[:].rearrange("p (c i t) -> p c t i", i=4, t=PACK),
                     wvd_raw[a, g].rearrange("p t (c i) -> p c t i", i=4),
                 )
                 codes = keep.tile([P, GROUP], U32, name="wd_codes_%d_%d" % (g, a), align_bytes=64)
-                sc = keep.tile([P, GROUP], U8, name="wd_sc_%d_%d" % (g, a), align_bytes=64)
-                nc.vector.quantize_mx(codes[:].bitcast(FP8X4), sc[:], grouped[:])
-                wd_codes[g, a], wd_sc[g, a] = codes, sc
+                scales = keep.tile([P, GROUP], U8, name="wd_sc_%d_%d" % (g, a), align_bytes=64)
+                nc.vector.quantize_mx(codes[:].bitcast(FP8X4), scales[:], grouped[:])
+                wd_codes[g, a], wd_sc[g, a] = codes, scales
 
-        def fp4_passes(acc, words, plane, i, h, last):
-            c = i * P
+        def fp4_passes(acc, words, plane, i, h, closes):
             for a in range(PASSES):
                 nc.tensor.matmul_mx(
                     acc[:],
-                    lhsT=words[:, a, 2 * c : 2 * (c + P)].bitcast(FP4X4),
+                    lhsT=words[:, a, 2 * i * P : 2 * (i + 1) * P].bitcast(FP4X4),
                     lhsT_scale=plane[:, a, i * P : (i + 1) * P],
-                    rhs=v_w[h, a][:].bitcast(FP4X4),
+                    rhs=v_w[h, a].bitcast(FP4X4),
                     rhs_scale=v_sc[h, a],
                     start=(a == 0),
-                    stop=(last and a == PASSES - 1),
+                    stop=(closes and a == PASSES - 1),
                 )
 
         def fp8_passes(acc, i, h):
-            c = (i % 2) * P
+            g, c = divmod(i * P, GROUP)
             for a in range(PASSES):
                 nc.tensor.matmul_mx(
                     acc[:],
-                    lhsT=wd_codes[i // 2, a][:, c : c + P].bitcast(FP8X4),
-                    lhsT_scale=wd_sc[i // 2, a][:, c : c + P],
-                    rhs=v_w[h, a][:].bitcast(FP4X4),
+                    lhsT=wd_codes[g, a][:, c : c + P].bitcast(FP8X4),
+                    lhsT_scale=wd_sc[g, a][:, c : c + P],
+                    rhs=v_w[h, a].bitcast(FP4X4),
                     rhs_scale=v_sc[h, a],
                     start=False,
                     stop=(a == PASSES - 1),
                 )
 
         def key(i, h):
-            gate = st_sb[i][:, h * JH : (h + 1) * JH]
-            ke = psum.tile([P, JH], F32, name="ke")
+            gate = st_sb[i][:, h * HALF : (h + 1) * HALF]
+            ke = psum.tile([P, HALF], F32, name="ke")
             fp4_passes(ke, wk_w, wk_sc, i, h, True)
             nc.vector.tensor_tensor(gate, gate, ke[:], ADD)
             nc.scalar.activation(gate, gate, SIGMOID)
 
         def value(i, h):
-            gate = st_sb[i][:, h * JH : (h + 1) * JH]
-            ve = psum.tile([P, JH], F32, name="ve")
+            gate = st_sb[i][:, h * HALF : (h + 1) * HALF]
+            ve = psum.tile([P, HALF], F32, name="ve")
             fp4_passes(ve, wv_w, wv_sc, i, h, False)
             fp8_passes(ve, i, h)
             nc.vector.tensor_tensor(gate, gate, ve[:], MULT)
 
         def finish(i, h):
-            cols = slice(h * JH, (h + 1) * JH)
-            adder = nc.gpsimd if 2 * i + h < 14 else nc.vector
+            cols = slice(h * HALF, (h + 1) * HALF)
+            adder = nc.vector if (i, h) in VECTOR_ADDS else nc.gpsimd
             adder.tensor_tensor(res_sb[i][:, cols], res_sb[i][:, cols], st_sb[i][:, cols], ADD)
-            if i == N_TILES - 1:
+            if i == ROW_TILES - 1:
                 nc.sync.dma_start(out[i * P : (i + 1) * P, cols], res_sb[i][:, cols])
             elif h == 1:
                 nc.sync.dma_start(out[i * P : (i + 1) * P, :], res_sb[i][:])
 
-        units = [(0, 0), (1, 0), (0, 1), (1, 1)] + [(i, h) for i in range(2, N_TILES) for h in range(2)]
-        gather(0)
+        units = [(0, 0), (1, 0), (0, 1), (1, 1)] + [(i, h) for i in range(2, ROW_TILES) for h in range(2)]
+        units_per_group = 2 * GROUP // P
+        gather_first_half()
         quantise(0)
-        gather(1)
-        key(*units[0])
+        gather_second_half()
+        for unit in units[:KEYS_AHEAD]:
+            key(*unit)
         for u, (i, h) in enumerate(units):
-            if u % 4 == 2 and u // 4 + 1 < N // GROUP:
-                quantise(u // 4 + 1)
-            if u + 1 < len(units):
-                key(*units[u + 1])
+            g, place = divmod(u, units_per_group)
+            if place == 0 and g + 1 < N // GROUP:
+                quantise(g + 1)
+            if u + KEYS_AHEAD < len(units):
+                key(*units[u + KEYS_AHEAD])
             value(i, h)
             finish(i, h)

@@ -25,9 +25,10 @@ HALF = 512
 GROUP = 256
 ROW_TILES = N // P
 LIST_ROWS = 16
-BANKS = 4
-KEYS_AHEAD = 2
+KEY_BANKS, VALUE_BANKS = 4, 4
+PIECES = ((0, GROUP), (GROUP, 2 * GROUP), (2 * GROUP, N))
 VECTOR_ADDS = ((ROW_TILES - 2, 1), (ROW_TILES - 1, 1))
+KEYS_AHEAD = 2
 
 
 def tile_list_engram_dl_add_kernel(
@@ -36,7 +37,7 @@ def tile_list_engram_dl_add_kernel(
     nc = tc.nc
     with ExitStack() as ctx:
         keep = ctx.enter_context(tc.tile_pool(name="keep", bufs=1))
-        psum = ctx.enter_context(tc.psum_pool(name="psum", bufs=BANKS))
+        psum = ctx.enter_context(tc.psum_pool(name="psum", bufs=1))
 
         offsets = keep.tile([P, J // LIST_ROWS], U16, name="offsets")
         tab_sc = keep.tile([P, PASSES, T], U8, name="tab_sc", align_bytes=64)
@@ -64,36 +65,37 @@ def tile_list_engram_dl_add_kernel(
             raw = keep.tile([P, PACK, c1 - c0], F32, name="wvd_raw_%d_%d" % (a, c0), align_bytes=64)
             src = wvd[K_PASS * a : K_PASS * (a + 1), c0:c1].rearrange("(p t) n -> p t n", t=PACK)
             nc.sync.dma_start(raw[:], src)
-            for g in range(c0 // GROUP, c1 // GROUP):
-                wvd_raw[a, g] = raw[:, :, g * GROUP - c0 : (g + 1) * GROUP - c0]
+            for first, last in PIECES:
+                if c0 <= first and last <= c1:
+                    wvd_raw[a, first] = raw[:, :, first - c0 : last - c0]
 
-        def load_rows(name, dram, tiles, indices):
-            for i in indices:
-                tiles[i] = keep.tile([P, J], F32, name="%s_%d" % (name, i), align_bytes=64)
-                nc.sync.dma_start(tiles[i][:], dram[P * i : P * (i + 1), :])
+        def rows_of(dram, first, count):
+            return dram[P * first : P * (first + count), :].rearrange("(i p) j -> p i j", p=P)
+
+        def load_rows(name, dram, tiles, first, count):
+            held = keep.tile([P, count, J], F32, name="%s_%d" % (name, first), align_bytes=64)
+            nc.sync.dma_start(held[:], rows_of(dram, first, count))
+            for i in range(count):
+                tiles[first + i] = held[:, i, :]
+            return held
 
         nc.sync.dma_start(offsets[:], offs)
         wk_w = load_words("wk_w", wk_words)
         load_scales(nc.sync, tab_sc, tab_scales)
         load_scales(nc.gpsimd, wv_sc, wv4_scales)
         nc.sync.dma_start(tab_w[:], tab_words[0].rearrange("p t b -> p (t b)").bitcast(I32))
-        load_wvd(0, 0, GROUP)
-        wv_w = load_words("wv_w", wv4_words)
         load_scales(nc.sync, wk_sc, wk_scales)
-        load_wvd(0, GROUP, 2 * GROUP)
-        load_rows("res", res, res_sb, [0])
-        load_wvd(1, 0, 2 * GROUP)
-        load_rows("st", st, st_sb, [0, 1])
-        load_wvd(0, 2 * GROUP, 3 * GROUP)
-        load_rows("st", st, st_sb, [2])
-        load_rows("res", res, res_sb, [1, 2])
-        load_wvd(0, 3 * GROUP, 4 * GROUP)
-        load_rows("st", st, st_sb, [3])
-        load_wvd(1, 2 * GROUP, 4 * GROUP)
-        load_rows("st", st, st_sb, [4, 5])
-        load_rows("res", res, res_sb, [3, 4, 5, 6])
-        load_rows("st", st, st_sb, [6, 7])
-        load_rows("res", res, res_sb, [7])
+        wv_w = load_words("wv_w", wv4_words)
+        load_wvd(0, 0, N)
+        load_rows("st", st, st_sb, 0, 1)
+        load_wvd(1, 0, GROUP)
+        load_rows("st", st, st_sb, 1, 1)
+        load_rows("res", res, res_sb, 0, 1)
+        load_wvd(1, GROUP, N)
+        for i in range(1, ROW_TILES):
+            if i + 1 < ROW_TILES:
+                load_rows("st", st, st_sb, i + 1, 1)
+            load_rows("res", res, res_sb, i, 1)
 
         v_w, v_sc = {}, {}
 
@@ -134,17 +136,21 @@ def tile_list_engram_dl_add_kernel(
 
         wd_codes, wd_sc = {}, {}
 
-        def quantise(g):
+        def quantise(first, last):
+            width = last - first
             for a in range(PASSES):
-                grouped = keep.tile([P, GROUP * PACK], BF16, name="grouped_%d_%d" % (g, a), align_bytes=64)
-                nc.scalar.copy(
+                grouped = keep.tile([P, width * PACK], BF16, name="grouped_%d_%d" % (first, a), align_bytes=64)
+                rounder = nc.vector.tensor_copy if (first, a) == (0, PASSES - 1) else nc.scalar.copy
+                rounder(
                     grouped[:].rearrange("p (c i t) -> p c t i", i=4, t=PACK),
-                    wvd_raw[a, g].rearrange("p t (c i) -> p c t i", i=4),
+                    wvd_raw[a, first].rearrange("p t (c i) -> p c t i", i=4),
                 )
-                codes = keep.tile([P, GROUP], U32, name="wd_codes_%d_%d" % (g, a), align_bytes=64)
-                scales = keep.tile([P, GROUP], U8, name="wd_sc_%d_%d" % (g, a), align_bytes=64)
+                codes = keep.tile([P, width], U32, name="wd_codes_%d_%d" % (first, a), align_bytes=64)
+                scales = keep.tile([P, width], U8, name="wd_sc_%d_%d" % (first, a), align_bytes=64)
                 nc.vector.quantize_mx(codes[:].bitcast(FP8X4), scales[:], grouped[:])
-                wd_codes[g, a], wd_sc[g, a] = codes, scales
+                for i in range(first // P, last // P):
+                    cols = slice(i * P - first, (i + 1) * P - first)
+                    wd_codes[i, a], wd_sc[i, a] = codes[:, cols], scales[:, cols]
 
         def fp4_passes(acc, words, plane, i, h, closes):
             for a in range(PASSES):
@@ -158,31 +164,30 @@ def tile_list_engram_dl_add_kernel(
                     stop=(closes and a == PASSES - 1),
                 )
 
-        def fp8_passes(acc, i, h):
-            g, c = divmod(i * P, GROUP)
-            for a in range(PASSES):
-                nc.tensor.matmul_mx(
-                    acc[:],
-                    lhsT=wd_codes[g, a][:, c : c + P].bitcast(FP8X4),
-                    lhsT_scale=wd_sc[g, a][:, c : c + P],
-                    rhs=v_w[h, a].bitcast(FP4X4),
-                    rhs_scale=v_sc[h, a],
-                    start=False,
-                    stop=(a == PASSES - 1),
-                )
+        def fp8_pass(acc, i, h, a):
+            nc.tensor.matmul_mx(
+                acc[:],
+                lhsT=wd_codes[i, a].bitcast(FP8X4),
+                lhsT_scale=wd_sc[i, a],
+                rhs=v_w[h, a].bitcast(FP4X4),
+                rhs_scale=v_sc[h, a],
+                start=False,
+                stop=(a == PASSES - 1),
+            )
 
         def key(i, h):
             gate = st_sb[i][:, h * HALF : (h + 1) * HALF]
-            ke = psum.tile([P, HALF], F32, name="ke")
+            ke = psum.tile([P, HALF], F32, name="ke", bufs=KEY_BANKS)
             fp4_passes(ke, wk_w, wk_sc, i, h, True)
             nc.vector.tensor_tensor(gate, gate, ke[:], ADD)
             nc.scalar.activation(gate, gate, SIGMOID)
 
         def value(i, h):
             gate = st_sb[i][:, h * HALF : (h + 1) * HALF]
-            ve = psum.tile([P, HALF], F32, name="ve")
+            ve = psum.tile([P, HALF], F32, name="ve", bufs=VALUE_BANKS)
             fp4_passes(ve, wv_w, wv_sc, i, h, False)
-            fp8_passes(ve, i, h)
+            fp8_pass(ve, i, h, 0)
+            fp8_pass(ve, i, h, 1)
             nc.vector.tensor_tensor(gate, gate, ve[:], MULT)
 
         def finish(i, h):
@@ -192,19 +197,17 @@ def tile_list_engram_dl_add_kernel(
             if i == ROW_TILES - 1:
                 nc.sync.dma_start(out[i * P : (i + 1) * P, cols], res_sb[i][:, cols])
             elif h == 1:
-                nc.sync.dma_start(out[i * P : (i + 1) * P, :], res_sb[i][:])
+                nc.sync.dma_start(out[i * P : (i + 1) * P, :], res_sb[i])
 
         units = [(0, 0), (1, 0), (0, 1), (1, 1)] + [(i, h) for i in range(2, ROW_TILES) for h in range(2)]
-        units_per_group = 2 * GROUP // P
         gather_first_half()
-        quantise(0)
         gather_second_half()
         for unit in units[:KEYS_AHEAD]:
             key(*unit)
+        quantise(*PIECES[0])
         for u, (i, h) in enumerate(units):
-            g, place = divmod(u, units_per_group)
-            if place == 0 and g + 1 < N // GROUP:
-                quantise(g + 1)
+            if u in (1, 3):
+                quantise(*PIECES[(u + 1) // 2])
             if u + KEYS_AHEAD < len(units):
                 key(*units[u + KEYS_AHEAD])
             value(i, h)

@@ -82,20 +82,25 @@ def tile_list_engram_dl_add_kernel(
         nc.sync.dma_start(offsets[:], offs)
         wk_w = load_words("wk_w", wk_words)
         load_scales(nc.sync, tab_sc, tab_scales)
-        load_scales(nc.gpsimd, wv_sc, wv4_scales)
         nc.sync.dma_start(tab_w[:], tab_words[0].rearrange("p t b -> p (t b)").bitcast(I32))
         load_scales(nc.sync, wk_sc, wk_scales)
         wv_w = load_words("wv_w", wv4_words)
+        load_scales(nc.sync, wv_sc, wv4_scales)
         load_wvd(0, 0, N)
         load_rows("st", st, st_sb, 0, 1)
         load_wvd(1, 0, GROUP)
         load_rows("st", st, st_sb, 1, 1)
-        load_rows("res", res, res_sb, 0, 1)
+        stored = {}
+
+        def load_res(first, count):
+            stored[first + count - 1] = (first, count, load_rows("res", res, res_sb, first, count))
+
+        load_res(0, 1)
         load_wvd(1, GROUP, N)
-        for i in range(1, ROW_TILES):
-            if i + 1 < ROW_TILES:
-                load_rows("st", st, st_sb, i + 1, 1)
-            load_rows("res", res, res_sb, i, 1)
+        for i in range(2, ROW_TILES, 2):
+            load_rows("st", st, st_sb, i, 2)
+            load_res(i - 1, 2)
+        load_res(ROW_TILES - 1, 1)
 
         v_w, v_sc = {}, {}
 
@@ -196,8 +201,11 @@ def tile_list_engram_dl_add_kernel(
             adder.tensor_tensor(res_sb[i][:, cols], res_sb[i][:, cols], st_sb[i][:, cols], ADD)
             if i == ROW_TILES - 1:
                 nc.sync.dma_start(out[i * P : (i + 1) * P, cols], res_sb[i][:, cols])
-            elif h == 1:
+            elif h == 1 and i >= ROW_TILES - 3:
                 nc.sync.dma_start(out[i * P : (i + 1) * P, :], res_sb[i])
+            elif h == 1 and i in stored:
+                first, count, held = stored[i]
+                nc.sync.dma_start(rows_of(out, first, count), held[:])
 
         units = [(0, 0), (1, 0), (0, 1), (1, 1)] + [(i, h) for i in range(2, ROW_TILES) for h in range(2)]
         gather_first_half()

@@ -27,7 +27,8 @@ ROW_TILES = N // P
 LIST_ROWS = 16
 KEY_BANKS, VALUE_BANKS = 4, 4
 PIECES = ((0, GROUP), (GROUP, 2 * GROUP), (2 * GROUP, N))
-VECTOR_ADDS = ((ROW_TILES - 2, 1), (ROW_TILES - 1, 1))
+VECTOR_ADDS = ((ROW_TILES - 1, 0), (ROW_TILES - 1, 1))
+EARLY = 4
 KEYS_AHEAD = 2
 
 
@@ -79,28 +80,35 @@ def tile_list_engram_dl_add_kernel(
                 tiles[first + i] = held[:, i, :]
             return held
 
+        def hold_early(name, tiles):
+            held = keep.tile([P, EARLY, J], F32, name=name, align_bytes=64)
+            for i in range(EARLY):
+                tiles[i] = held[:, i, :]
+            return held
+
+        def load_half(held, dram, h):
+            cols = slice(h * HALF, (h + 1) * HALF)
+            nc.sync.dma_start(held[:, :, cols], rows_of(dram, 0, EARLY)[:, :, cols])
+
         nc.sync.dma_start(offsets[:], offs)
         wk_w = load_words("wk_w", wk_words)
         load_scales(nc.sync, tab_sc, tab_scales)
         nc.sync.dma_start(tab_w[:], tab_words[0].rearrange("p t b -> p (t b)").bitcast(I32))
-        load_scales(nc.sync, wk_sc, wk_scales)
         wv_w = load_words("wv_w", wv4_words)
+        load_scales(nc.sync, wk_sc, wk_scales)
+        load_wvd(0, 0, N // 2)
         load_scales(nc.sync, wv_sc, wv4_scales)
-        load_wvd(0, 0, N)
-        load_rows("st", st, st_sb, 0, 1)
-        load_wvd(1, 0, GROUP)
-        load_rows("st", st, st_sb, 1, 1)
-        stored = {}
-
-        def load_res(first, count):
-            stored[first + count - 1] = (first, count, load_rows("res", res, res_sb, first, count))
-
-        load_res(0, 1)
-        load_wvd(1, GROUP, N)
-        for i in range(2, ROW_TILES, 2):
+        load_wvd(1, 0, N // 2)
+        st_early, res_early = hold_early("st_early", st_sb), hold_early("res_early", res_sb)
+        load_half(st_early, st, 0)
+        load_half(st_early, st, 1)
+        load_half(res_early, res, 0)
+        load_wvd(0, N // 2, N)
+        load_wvd(1, N // 2, N)
+        load_half(res_early, res, 1)
+        for i in range(EARLY, ROW_TILES, 2):
             load_rows("st", st, st_sb, i, 2)
-            load_res(i - 1, 2)
-        load_res(ROW_TILES - 1, 1)
+            load_rows("res", res, res_sb, i, 2)
 
         v_w, v_sc = {}, {}
 
@@ -145,8 +153,7 @@ def tile_list_engram_dl_add_kernel(
             width = last - first
             for a in range(PASSES):
                 grouped = keep.tile([P, width * PACK], BF16, name="grouped_%d_%d" % (first, a), align_bytes=64)
-                rounder = nc.vector.tensor_copy if (first, a) == (0, PASSES - 1) else nc.scalar.copy
-                rounder(
+                nc.scalar.copy(
                     grouped[:].rearrange("p (c i t) -> p c t i", i=4, t=PACK),
                     wvd_raw[a, first].rearrange("p t (c i) -> p c t i", i=4),
                 )
@@ -201,21 +208,19 @@ def tile_list_engram_dl_add_kernel(
             adder.tensor_tensor(res_sb[i][:, cols], res_sb[i][:, cols], st_sb[i][:, cols], ADD)
             if i == ROW_TILES - 1:
                 nc.sync.dma_start(out[i * P : (i + 1) * P, cols], res_sb[i][:, cols])
-            elif h == 1 and i >= ROW_TILES - 3:
+            elif h == 1:
                 nc.sync.dma_start(out[i * P : (i + 1) * P, :], res_sb[i])
-            elif h == 1 and i in stored:
-                first, count, held = stored[i]
-                nc.sync.dma_start(rows_of(out, first, count), held[:])
 
-        units = [(0, 0), (1, 0), (0, 1), (1, 1)] + [(i, h) for i in range(2, ROW_TILES) for h in range(2)]
+        units = [(i, h) for h in range(2) for i in range(4)] + [(i, h) for i in range(4, ROW_TILES) for h in range(2)]
         gather_first_half()
         gather_second_half()
         for unit in units[:KEYS_AHEAD]:
             key(*unit)
         quantise(*PIECES[0])
+        quantise(*PIECES[1])
         for u, (i, h) in enumerate(units):
-            if u in (1, 3):
-                quantise(*PIECES[(u + 1) // 2])
+            if u == 4:
+                quantise(*PIECES[2])
             if u + KEYS_AHEAD < len(units):
                 key(*units[u + KEYS_AHEAD])
             value(i, h)

@@ -26,7 +26,7 @@ GROUP = 256
 ROW_TILES = N // P
 LIST_ROWS = 16
 KEY_BANKS, VALUE_BANKS = 4, 4
-PIECES = ((0, GROUP), (GROUP, 2 * GROUP), (2 * GROUP, N))
+PIECES = tuple((c, c + GROUP) for c in range(0, N, GROUP))
 VECTOR_ADDS = ((ROW_TILES - 1, 0), (ROW_TILES - 1, 1))
 EARLY = 4
 KEYS_AHEAD = 2
@@ -103,12 +103,15 @@ def tile_list_engram_dl_add_kernel(
         load_half(st_early, st, 0)
         load_half(st_early, st, 1)
         load_half(res_early, res, 0)
-        load_wvd(0, N // 2, N)
-        load_wvd(1, N // 2, N)
+        for a in range(PASSES):
+            load_wvd(a, *PIECES[2])
         load_half(res_early, res, 1)
-        for i in range(EARLY, ROW_TILES, 2):
-            load_rows("st", st, st_sb, i, 2)
-            load_rows("res", res, res_sb, i, 2)
+        load_rows("st", st, st_sb, EARLY, 2)
+        for a in range(PASSES):
+            load_wvd(a, *PIECES[3])
+        load_rows("res", res, res_sb, EARLY, 2)
+        load_rows("st", st, st_sb, EARLY + 2, 2)
+        load_rows("res", res, res_sb, EARLY + 2, 2)
 
         v_w, v_sc = {}, {}
 
@@ -164,42 +167,49 @@ def tile_list_engram_dl_add_kernel(
                     cols = slice(i * P - first, (i + 1) * P - first)
                     wd_codes[i, a], wd_sc[i, a] = codes[:, cols], scales[:, cols]
 
-        def fp4_passes(acc, words, plane, i, h, closes):
-            for a in range(PASSES):
-                nc.tensor.matmul_mx(
-                    acc[:],
-                    lhsT=words[:, a, 2 * i * P : 2 * (i + 1) * P].bitcast(FP4X4),
-                    lhsT_scale=plane[:, a, i * P : (i + 1) * P],
-                    rhs=v_w[h, a].bitcast(FP4X4),
-                    rhs_scale=v_sc[h, a],
-                    start=(a == 0),
-                    stop=(closes and a == PASSES - 1),
-                )
+        def fp4_pass(acc, words, plane, i, h, a, start, stop):
+            nc.tensor.matmul_mx(
+                acc[:],
+                lhsT=words[:, a, 2 * i * P : 2 * (i + 1) * P].bitcast(FP4X4),
+                lhsT_scale=plane[:, a, i * P : (i + 1) * P],
+                rhs=v_w[h, a].bitcast(FP4X4),
+                rhs_scale=v_sc[h, a],
+                start=start,
+                stop=stop,
+            )
 
-        def fp8_pass(acc, i, h, a):
+        def fp8_pass(acc, i, h, a, start, stop):
             nc.tensor.matmul_mx(
                 acc[:],
                 lhsT=wd_codes[i, a].bitcast(FP8X4),
                 lhsT_scale=wd_sc[i, a],
                 rhs=v_w[h, a].bitcast(FP4X4),
                 rhs_scale=v_sc[h, a],
-                start=False,
-                stop=(a == PASSES - 1),
+                start=start,
+                stop=stop,
             )
 
         def key(i, h):
             gate = st_sb[i][:, h * HALF : (h + 1) * HALF]
             ke = psum.tile([P, HALF], F32, name="ke", bufs=KEY_BANKS)
-            fp4_passes(ke, wk_w, wk_sc, i, h, True)
+            for a in range(PASSES):
+                fp4_pass(ke, wk_w, wk_sc, i, h, a, a == 0, a == PASSES - 1)
             nc.vector.tensor_tensor(gate, gate, ke[:], ADD)
             nc.scalar.activation(gate, gate, SIGMOID)
 
         def value(i, h):
             gate = st_sb[i][:, h * HALF : (h + 1) * HALF]
             ve = psum.tile([P, HALF], F32, name="ve", bufs=VALUE_BANKS)
-            fp4_passes(ve, wv_w, wv_sc, i, h, False)
-            fp8_pass(ve, i, h, 0)
-            fp8_pass(ve, i, h, 1)
+            if i < EARLY:
+                for a in range(PASSES):
+                    fp4_pass(ve, wv_w, wv_sc, i, h, a, a == 0, False)
+                for a in range(PASSES):
+                    fp8_pass(ve, i, h, a, False, a == PASSES - 1)
+            else:
+                for a in reversed(range(PASSES)):
+                    fp8_pass(ve, i, h, a, a == PASSES - 1, False)
+                for a in range(PASSES):
+                    fp4_pass(ve, wv_w, wv_sc, i, h, a, False, a == PASSES - 1)
             nc.vector.tensor_tensor(gate, gate, ve[:], MULT)
 
         def finish(i, h):
@@ -219,8 +229,8 @@ def tile_list_engram_dl_add_kernel(
         quantise(*PIECES[0])
         quantise(*PIECES[1])
         for u, (i, h) in enumerate(units):
-            if u == 4:
-                quantise(*PIECES[2])
+            if u in (4, 8):
+                quantise(*PIECES[u // 4 + 1])
             if u + KEYS_AHEAD < len(units):
                 key(*units[u + KEYS_AHEAD])
             value(i, h)

@@ -50,6 +50,10 @@ def tile_list_engram_dl_add_kernel(
         nc.vector.memset(wk_sc[:].bitcast(I32), 0)
         nc.gpsimd.memset(wv_sc[:].bitcast(I32), 0)
 
+        warm = keep.tile([P, 1], F32, name="warm")
+        nc.gpsimd.memset(warm[:], 0.0)
+        nc.scalar.activation(warm[:], warm[:], SIGMOID)
+
         wvd_raw, st_sb, res_sb = {}, {}, {}
 
         def load_scales(queue, plane, dram):
@@ -80,16 +84,6 @@ def tile_list_engram_dl_add_kernel(
                 tiles[first + i] = held[:, i, :]
             return held
 
-        def hold_early(name, tiles):
-            held = keep.tile([P, EARLY, J], F32, name=name, align_bytes=64)
-            for i in range(EARLY):
-                tiles[i] = held[:, i, :]
-            return held
-
-        def load_half(held, dram, h):
-            cols = slice(h * HALF, (h + 1) * HALF)
-            nc.sync.dma_start(held[:, :, cols], rows_of(dram, 0, EARLY)[:, :, cols])
-
         nc.sync.dma_start(offsets[:], offs)
         wk_w = load_words("wk_w", wk_words)
         load_scales(nc.sync, tab_sc, tab_scales)
@@ -99,19 +93,17 @@ def tile_list_engram_dl_add_kernel(
         load_wvd(0, 0, N // 2)
         load_scales(nc.sync, wv_sc, wv4_scales)
         load_wvd(1, 0, N // 2)
-        st_early, res_early = hold_early("st_early", st_sb), hold_early("res_early", res_sb)
-        load_half(st_early, st, 0)
-        load_half(st_early, st, 1)
-        load_half(res_early, res, 0)
-        for a in range(PASSES):
-            load_wvd(a, *PIECES[2])
-        load_half(res_early, res, 1)
-        load_rows("st", st, st_sb, EARLY, 2)
-        for a in range(PASSES):
-            load_wvd(a, *PIECES[3])
-        load_rows("res", res, res_sb, EARLY, 2)
-        load_rows("st", st, st_sb, EARLY + 2, 2)
-        load_rows("res", res, res_sb, EARLY + 2, 2)
+        load_rows("st", st, st_sb, 0, 2)
+        load_rows("st", st, st_sb, 2, 1)
+        load_rows("st", st, st_sb, 3, 1)
+        load_rows("res", res, res_sb, 0, 2)
+        load_wvd(0, N // 2, N)
+        load_wvd(1, N // 2, N)
+        load_rows("res", res, res_sb, 2, 2)
+        load_rows("st", st, st_sb, 4, 2)
+        load_rows("res", res, res_sb, 4, 2)
+        load_rows("st", st, st_sb, 6, 2)
+        load_rows("res", res, res_sb, 6, 2)
 
         v_w, v_sc = {}, {}
 
@@ -119,7 +111,7 @@ def tile_list_engram_dl_add_kernel(
             return offsets[:, h * (HALF // LIST_ROWS) : (h + 1) * (HALF // LIST_ROWS)]
 
         def gather_scales(h, a, planes):
-            v_sc[h, a] = planes[:, a * HALF : (a + 1) * HALF]
+            v_sc[h, a] = planes
             nc.vector.tensor_copy(v_sc[h, a], tab_sc[:, a, :].indirect(picks(h)))
 
         def gather_words(h, both):
@@ -136,36 +128,36 @@ def tile_list_engram_dl_add_kernel(
             planes = keep.tile([P, PASSES * HALF], U8, name="planes0", align_bytes=64)
             parted, paired = by_pass(0, both[:])
             for a in range(PASSES):
-                gather_scales(0, a, planes[:])
+                gather_scales(0, a, planes[:, a * HALF : (a + 1) * HALF])
             gather_words(0, both[:])
             for a in range(PASSES):
                 nc.vector.tensor_copy(parted[:, a, :], paired[:, a, :])
 
         def gather_second_half():
-            picked = keep.tile([P, 6 * HALF], U8, name="picked1", tag="picked", align_bytes=64)
-            both, planes = picked[:, : 4 * HALF], picked[:, 4 * HALF :]
+            picked = keep.tile([P, 5 * HALF], U8, name="picked1", tag="picked", align_bytes=64)
+            both = picked[:, : 4 * HALF]
             parted, paired = by_pass(1, both)
             gather_words(1, both)
-            gather_scales(1, 0, planes)
+            gather_scales(1, 0, picked[:, 4 * HALF :])
             nc.vector.tensor_copy(parted, paired)
-            gather_scales(1, 1, planes)
+            last = keep.tile([P, HALF], U8, name="last_plane", tag="stage00", align_bytes=64)
+            gather_scales(1, 1, last[:])
 
         wd_codes, wd_sc = {}, {}
 
-        def quantise(first, last):
-            width = last - first
-            for a in range(PASSES):
-                grouped = keep.tile([P, width * PACK], BF16, name="grouped_%d_%d" % (first, a), align_bytes=64)
-                nc.scalar.copy(
-                    grouped[:].rearrange("p (c i t) -> p c t i", i=4, t=PACK),
-                    wvd_raw[a, first].rearrange("p t (c i) -> p c t i", i=4),
-                )
-                codes = keep.tile([P, width], U32, name="wd_codes_%d_%d" % (first, a), align_bytes=64)
-                scales = keep.tile([P, width], U8, name="wd_sc_%d_%d" % (first, a), align_bytes=64)
-                nc.vector.quantize_mx(codes[:].bitcast(FP8X4), scales[:], grouped[:])
-                for i in range(first // P, last // P):
-                    cols = slice(i * P - first, (i + 1) * P - first)
-                    wd_codes[i, a], wd_sc[i, a] = codes[:, cols], scales[:, cols]
+        def quantise(g, a, stage, copy):
+            first, last = PIECES[g]
+            grouped = keep.tile([P, GROUP * PACK], BF16, name="grouped_%d_%d" % (g, a), tag=stage, align_bytes=64)
+            copy(
+                grouped[:].rearrange("p (c i t) -> p c t i", i=4, t=PACK),
+                wvd_raw[a, first].rearrange("p t (c i) -> p c t i", i=4),
+            )
+            codes = keep.tile([P, GROUP], U32, name="wd_codes_%d_%d" % (g, a), align_bytes=64)
+            scales = keep.tile([P, GROUP], U8, name="wd_sc_%d_%d" % (g, a), align_bytes=64)
+            nc.vector.quantize_mx(codes[:].bitcast(FP8X4), scales[:], grouped[:])
+            for i in range(first // P, last // P):
+                cols = slice(i * P - first, (i + 1) * P - first)
+                wd_codes[i, a], wd_sc[i, a] = codes[:, cols], scales[:, cols]
 
         def fp4_pass(acc, words, plane, i, h, a, start, stop):
             nc.tensor.matmul_mx(
@@ -189,18 +181,21 @@ def tile_list_engram_dl_add_kernel(
                 stop=stop,
             )
 
-        def key(i, h):
+        def bank(number):
+            return psum.tile([P, HALF], F32, name="bank%d" % number, bufs=1)
+
+        def key(i, h, number):
             gate = st_sb[i][:, h * HALF : (h + 1) * HALF]
-            ke = psum.tile([P, HALF], F32, name="ke", bufs=KEY_BANKS)
+            ke = bank(number)
             for a in range(PASSES):
                 fp4_pass(ke, wk_w, wk_sc, i, h, a, a == 0, a == PASSES - 1)
             nc.vector.tensor_tensor(gate, gate, ke[:], ADD)
             nc.scalar.activation(gate, gate, SIGMOID)
 
-        def value(i, h):
+        def value(i, h, number):
             gate = st_sb[i][:, h * HALF : (h + 1) * HALF]
-            ve = psum.tile([P, HALF], F32, name="ve", bufs=VALUE_BANKS)
-            if i < EARLY:
+            ve = bank(number)
+            if i <= EARLY:
                 for a in range(PASSES):
                     fp4_pass(ve, wv_w, wv_sc, i, h, a, a == 0, False)
                 for a in range(PASSES):
@@ -223,15 +218,18 @@ def tile_list_engram_dl_add_kernel(
 
         units = [(i, h) for h in range(2) for i in range(4)] + [(i, h) for i in range(4, ROW_TILES) for h in range(2)]
         gather_first_half()
+        quantise(0, 0, "stage00", nc.scalar.copy)
         gather_second_half()
-        for unit in units[:KEYS_AHEAD]:
-            key(*unit)
-        quantise(*PIECES[0])
-        quantise(*PIECES[1])
+        banks = [(0, 4), (1, 5), (2, 6), (3, 7)] + [(1, 0), (4, 5), (2, 6), (3, 7)] * 3
+        for u in range(KEYS_AHEAD):
+            key(*units[u], banks[u][0])
+        for g, a in ((0, 1), (1, 0), (1, 1)):
+            quantise(g, a, "stage%d%d" % (g, a), nc.scalar.copy)
         for u, (i, h) in enumerate(units):
             if u in (4, 8):
-                quantise(*PIECES[u // 4 + 1])
+                quantise(u // 4 + 1, 0, "stage20" if u == 4 else "stage21", nc.scalar.copy)
+                quantise(u // 4 + 1, 1, "stage21" if u == 4 else "stage20", nc.scalar.copy)
             if u + KEYS_AHEAD < len(units):
-                key(*units[u + KEYS_AHEAD])
-            value(i, h)
+                key(*units[u + KEYS_AHEAD], banks[u + KEYS_AHEAD][0])
+            value(i, h, banks[u][1])
             finish(i, h)

@@ -27,7 +27,7 @@ ROW_TILES = N // P
 LIST_ROWS = 16
 KEY_BANKS, VALUE_BANKS = 4, 4
 PIECES = tuple((c, c + GROUP) for c in range(0, N, GROUP))
-VECTOR_ADDS = ((ROW_TILES - 1, 0), (ROW_TILES - 1, 1))
+VECTOR_ADDS = ((ROW_TILES - 2, 1), (ROW_TILES - 1, 0), (ROW_TILES - 1, 1))
 EARLY = 4
 KEYS_AHEAD = 2
 
@@ -49,10 +49,6 @@ def tile_list_engram_dl_add_kernel(
         nc.vector.memset(tab_sc[:].bitcast(I32), 0)
         nc.vector.memset(wk_sc[:].bitcast(I32), 0)
         nc.gpsimd.memset(wv_sc[:].bitcast(I32), 0)
-
-        warm = keep.tile([P, 1], F32, name="warm")
-        nc.gpsimd.memset(warm[:], 0.0)
-        nc.scalar.activation(warm[:], warm[:], SIGMOID)
 
         wvd_raw, st_sb, res_sb = {}, {}, {}
 
@@ -84,22 +80,23 @@ def tile_list_engram_dl_add_kernel(
                 tiles[first + i] = held[:, i, :]
             return held
 
+        table = tab_words[0].rearrange("p t b -> p (t b)").bitcast(I32)
+        nc.sync.dma_start(tab_w[:, : T // 2], table[:, : T // 2])
         nc.sync.dma_start(offsets[:], offs)
-        wk_w = load_words("wk_w", wk_words)
         load_scales(nc.sync, tab_sc, tab_scales)
-        nc.sync.dma_start(tab_w[:], tab_words[0].rearrange("p t b -> p (t b)").bitcast(I32))
-        wv_w = load_words("wv_w", wv4_words)
+        nc.sync.dma_start(tab_w[:, T // 2 :], table[:, T // 2 :])
+        wk_w = load_words("wk_w", wk_words)
         load_scales(nc.sync, wk_sc, wk_scales)
+        wv_w = load_words("wv_w", wv4_words)
         load_wvd(0, 0, N // 2)
         load_scales(nc.sync, wv_sc, wv4_scales)
         load_wvd(1, 0, N // 2)
         load_rows("st", st, st_sb, 0, 2)
-        load_rows("st", st, st_sb, 2, 1)
-        load_rows("st", st, st_sb, 3, 1)
-        load_rows("res", res, res_sb, 0, 2)
+        load_rows("st", st, st_sb, 2, 2)
         load_wvd(0, N // 2, N)
+        res_pair = {0: load_rows("res", res, res_sb, 0, 2)}
         load_wvd(1, N // 2, N)
-        load_rows("res", res, res_sb, 2, 2)
+        res_pair[2] = load_rows("res", res, res_sb, 2, 2)
         load_rows("st", st, st_sb, 4, 2)
         load_rows("res", res, res_sb, 4, 2)
         load_rows("st", st, st_sb, 6, 2)
@@ -123,39 +120,40 @@ def tile_list_engram_dl_add_kernel(
                 v_w[h, a] = parted[:, a, :]
             return parted[:].bitcast(U16), both.bitcast(U16).rearrange("p (j d) -> p d j", d=PASSES)
 
-        def gather_first_half():
+        def gather_first_pass():
             both = keep.tile([P, 4 * HALF], U8, name="picked0", tag="picked", align_bytes=64)
-            planes = keep.tile([P, PASSES * HALF], U8, name="planes0", align_bytes=64)
+            plane = keep.tile([P, HALF], U8, name="plane00", align_bytes=64)
             parted, paired = by_pass(0, both[:])
-            for a in range(PASSES):
-                gather_scales(0, a, planes[:, a * HALF : (a + 1) * HALF])
+            gather_scales(0, 0, plane[:])
             gather_words(0, both[:])
             for a in range(PASSES):
                 nc.vector.tensor_copy(parted[:, a, :], paired[:, a, :])
 
-        def gather_second_half():
-            picked = keep.tile([P, 5 * HALF], U8, name="picked1", tag="picked", align_bytes=64)
+        def gather_rest():
+            picked = keep.tile([P, 6 * HALF], U8, name="picked1", tag="picked", align_bytes=64)
             both = picked[:, : 4 * HALF]
             parted, paired = by_pass(1, both)
+            gather_scales(0, 1, picked[:, 5 * HALF :])
             gather_words(1, both)
-            gather_scales(1, 0, picked[:, 4 * HALF :])
+            gather_scales(1, 0, picked[:, 4 * HALF : 5 * HALF])
             nc.vector.tensor_copy(parted, paired)
             last = keep.tile([P, HALF], U8, name="last_plane", tag="stage00", align_bytes=64)
             gather_scales(1, 1, last[:])
 
         wd_codes, wd_sc = {}, {}
 
-        def quantise(g, a, stage, copy):
-            first, last = PIECES[g]
-            grouped = keep.tile([P, GROUP * PACK], BF16, name="grouped_%d_%d" % (g, a), tag=stage, align_bytes=64)
-            copy(
-                grouped[:].rearrange("p (c i t) -> p c t i", i=4, t=PACK),
-                wvd_raw[a, first].rearrange("p t (c i) -> p c t i", i=4),
-            )
-            codes = keep.tile([P, GROUP], U32, name="wd_codes_%d_%d" % (g, a), align_bytes=64)
-            scales = keep.tile([P, GROUP], U8, name="wd_sc_%d_%d" % (g, a), align_bytes=64)
+        def quantise(groups, a, stage, copy):
+            first, width = PIECES[groups[0]][0], GROUP * len(groups)
+            grouped = keep.tile([P, width * PACK], BF16, name="grouped_%d_%d" % (first, a), tag=stage, align_bytes=64)
+            for place, g in enumerate(groups):
+                copy(
+                    grouped[:, place * GROUP * PACK : (place + 1) * GROUP * PACK].rearrange("p (c i t) -> p c t i", i=4, t=PACK),
+                    wvd_raw[a, PIECES[g][0]].rearrange("p t (c i) -> p c t i", i=4),
+                )
+            codes = keep.tile([P, width], U32, name="wd_codes_%d_%d" % (first, a), align_bytes=64)
+            scales = keep.tile([P, width], U8, name="wd_sc_%d_%d" % (first, a), align_bytes=64)
             nc.vector.quantize_mx(codes[:].bitcast(FP8X4), scales[:], grouped[:])
-            for i in range(first // P, last // P):
+            for i in range(first // P, (first + width) // P):
                 cols = slice(i * P - first, (i + 1) * P - first)
                 wd_codes[i, a], wd_sc[i, a] = codes[:, cols], scales[:, cols]
 
@@ -184,11 +182,18 @@ def tile_list_engram_dl_add_kernel(
         def bank(number):
             return psum.tile([P, HALF], F32, name="bank%d" % number, bufs=1)
 
+        opened = {}
+
+        def open_key(i, h, number):
+            opened[i, h] = bank(number)
+            fp4_pass(opened[i, h], wk_w, wk_sc, i, h, 0, True, False)
+
         def key(i, h, number):
             gate = st_sb[i][:, h * HALF : (h + 1) * HALF]
-            ke = bank(number)
-            for a in range(PASSES):
-                fp4_pass(ke, wk_w, wk_sc, i, h, a, a == 0, a == PASSES - 1)
+            if (i, h) not in opened:
+                open_key(i, h, number)
+            ke = opened[i, h]
+            fp4_pass(ke, wk_w, wk_sc, i, h, 1, False, True)
             nc.vector.tensor_tensor(gate, gate, ke[:], ADD)
             nc.scalar.activation(gate, gate, SIGMOID)
 
@@ -213,22 +218,26 @@ def tile_list_engram_dl_add_kernel(
             adder.tensor_tensor(res_sb[i][:, cols], res_sb[i][:, cols], st_sb[i][:, cols], ADD)
             if i == ROW_TILES - 1:
                 nc.sync.dma_start(out[i * P : (i + 1) * P, cols], res_sb[i][:, cols])
-            elif h == 1:
+            elif h == 1 and i >= EARLY:
                 nc.sync.dma_start(out[i * P : (i + 1) * P, :], res_sb[i])
+            elif h == 1 and i % 2 == 1:
+                nc.sync.dma_start(rows_of(out, i - 1, 2), res_pair[i - 1][:])
 
         units = [(i, h) for h in range(2) for i in range(4)] + [(i, h) for i in range(4, ROW_TILES) for h in range(2)]
-        gather_first_half()
-        quantise(0, 0, "stage00", nc.scalar.copy)
-        gather_second_half()
         banks = [(0, 4), (1, 5), (2, 6), (3, 7)] + [(1, 0), (4, 5), (2, 6), (3, 7)] * 3
+        gather_first_pass()
+        for u in range(EARLY):
+            open_key(*units[u], banks[u][0])
+        quantise([0], 0, "stage00", nc.scalar.copy)
+        gather_rest()
         for u in range(KEYS_AHEAD):
             key(*units[u], banks[u][0])
         for g, a in ((0, 1), (1, 0), (1, 1)):
-            quantise(g, a, "stage%d%d" % (g, a), nc.scalar.copy)
+            quantise([g], a, "stage%d%d" % (g, a), nc.scalar.copy)
         for u, (i, h) in enumerate(units):
-            if u in (4, 8):
-                quantise(u // 4 + 1, 0, "stage20" if u == 4 else "stage21", nc.scalar.copy)
-                quantise(u // 4 + 1, 1, "stage21" if u == 4 else "stage20", nc.scalar.copy)
+            if u == EARLY:
+                quantise([2, 3], 0, "stage20", nc.scalar.copy)
+                quantise([2, 3], 1, "stage21", nc.scalar.copy)
             if u + KEYS_AHEAD < len(units):
                 key(*units[u + KEYS_AHEAD], banks[u + KEYS_AHEAD][0])
             value(i, h, banks[u][1])

@@ -40,11 +40,11 @@ def tile_list_engram_dl_add_kernel(
         keep = ctx.enter_context(tc.tile_pool(name="keep", bufs=1))
         psum = ctx.enter_context(tc.psum_pool(name="psum", bufs=1))
 
-        offsets = keep.tile([P, J // LIST_ROWS], U16, name="offsets")
-        tab_sc = keep.tile([P, PASSES, T], U8, name="tab_sc", align_bytes=64)
-        wk_sc = keep.tile([P, PASSES, N], U8, name="wk_sc", align_bytes=64)
-        wv_sc = keep.tile([P, PASSES, N], U8, name="wv_sc", align_bytes=64)
-        tab_w = keep.tile([P, T], I32, name="tab_w", align_bytes=64)
+        offsets = keep.tile([P, J // LIST_ROWS], U16, name="offsets", align_bytes=256)
+        tab_sc = keep.tile([P, PASSES, T], U8, name="tab_sc", align_bytes=256)
+        wk_sc = keep.tile([P, PASSES, N], U8, name="wk_sc", align_bytes=256)
+        wv_sc = keep.tile([P, PASSES, N], U8, name="wv_sc", align_bytes=256)
+        tab_w = keep.tile([P, T], I32, name="tab_w", align_bytes=256)
 
         nc.vector.memset(tab_sc[:].bitcast(I32), 0)
         nc.vector.memset(wk_sc[:].bitcast(I32), 0)
@@ -58,12 +58,12 @@ def tile_list_engram_dl_add_kernel(
                 queue.dma_start(plane[r:P:32, :, :].bitcast(I32), rows[r].bitcast(I32))
 
         def load_words(name, dram):
-            words = keep.tile([P, PASSES, 2 * N], U8, name=name, align_bytes=64)
+            words = keep.tile([P, PASSES, 2 * N], U8, name=name, align_bytes=256)
             nc.sync.dma_start(words[:].bitcast(I32), dram.rearrange("a p b -> p a b").bitcast(I32))
             return words
 
         def load_wvd(a, c0, c1):
-            raw = keep.tile([P, PACK, c1 - c0], F32, name="wvd_raw_%d_%d" % (a, c0), align_bytes=64)
+            raw = keep.tile([P, PACK, c1 - c0], F32, name="wvd_raw_%d_%d" % (a, c0), align_bytes=256)
             src = wvd[K_PASS * a : K_PASS * (a + 1), c0:c1].rearrange("(p t) n -> p t n", t=PACK)
             nc.sync.dma_start(raw[:], src)
             for first, last in PIECES:
@@ -74,7 +74,7 @@ def tile_list_engram_dl_add_kernel(
             return dram[P * first : P * (first + count), :].rearrange("(i p) j -> p i j", p=P)
 
         def load_rows(name, dram, tiles, first, count):
-            held = keep.tile([P, count, J], F32, name="%s_%d" % (name, first), align_bytes=64)
+            held = keep.tile([P, count, J], F32, name="%s_%d" % (name, first), align_bytes=256)
             nc.sync.dma_start(held[:], rows_of(dram, first, count))
             for i in range(count):
                 tiles[first + i] = held[:, i, :]
@@ -115,14 +115,14 @@ def tile_list_engram_dl_add_kernel(
             nc.vector.tensor_copy(both.bitcast(U32), tab_w[:].bitcast(U32).indirect(picks(h)))
 
         def by_pass(h, both):
-            parted = keep.tile([P, PASSES, 2 * HALF], U8, name="v_w_%d" % h, align_bytes=64)
+            parted = keep.tile([P, PASSES, 2 * HALF], U8, name="v_w_%d" % h, align_bytes=256)
             for a in range(PASSES):
                 v_w[h, a] = parted[:, a, :]
             return parted[:].bitcast(U16), both.bitcast(U16).rearrange("p (j d) -> p d j", d=PASSES)
 
         def gather_first_pass():
-            both = keep.tile([P, 4 * HALF], U8, name="picked0", tag="picked", align_bytes=64)
-            plane = keep.tile([P, HALF], U8, name="plane00", align_bytes=64)
+            both = keep.tile([P, 4 * HALF], U8, name="picked0", tag="picked", align_bytes=256)
+            plane = keep.tile([P, HALF], U8, name="plane00", align_bytes=256)
             parted, paired = by_pass(0, both[:])
             gather_scales(0, 0, plane[:])
             gather_words(0, both[:])
@@ -130,28 +130,28 @@ def tile_list_engram_dl_add_kernel(
                 nc.vector.tensor_copy(parted[:, a, :], paired[:, a, :])
 
         def gather_rest():
-            picked = keep.tile([P, 6 * HALF], U8, name="picked1", tag="picked", align_bytes=64)
+            picked = keep.tile([P, 6 * HALF], U8, name="picked1", tag="picked", align_bytes=256)
             both = picked[:, : 4 * HALF]
             parted, paired = by_pass(1, both)
             gather_scales(0, 1, picked[:, 5 * HALF :])
             gather_words(1, both)
             gather_scales(1, 0, picked[:, 4 * HALF : 5 * HALF])
             nc.vector.tensor_copy(parted, paired)
-            last = keep.tile([P, HALF], U8, name="last_plane", tag="stage00", align_bytes=64)
+            last = keep.tile([P, HALF], U8, name="last_plane", tag="stage00", align_bytes=256)
             gather_scales(1, 1, last[:])
 
         wd_codes, wd_sc = {}, {}
 
         def quantise(groups, a, stage, copy):
             first, width = PIECES[groups[0]][0], GROUP * len(groups)
-            grouped = keep.tile([P, width * PACK], BF16, name="grouped_%d_%d" % (first, a), tag=stage, align_bytes=64)
+            grouped = keep.tile([P, width * PACK], BF16, name="grouped_%d_%d" % (first, a), tag=stage, align_bytes=256)
             for place, g in enumerate(groups):
                 copy(
                     grouped[:, place * GROUP * PACK : (place + 1) * GROUP * PACK].rearrange("p (c i t) -> p c t i", i=4, t=PACK),
                     wvd_raw[a, PIECES[g][0]].rearrange("p t (c i) -> p c t i", i=4),
                 )
-            codes = keep.tile([P, width], U32, name="wd_codes_%d_%d" % (first, a), align_bytes=64)
-            scales = keep.tile([P, width], U8, name="wd_sc_%d_%d" % (first, a), align_bytes=64)
+            codes = keep.tile([P, width], U32, name="wd_codes_%d_%d" % (first, a), align_bytes=256)
+            scales = keep.tile([P, width], U8, name="wd_sc_%d_%d" % (first, a), align_bytes=256)
             nc.vector.quantize_mx(codes[:].bitcast(FP8X4), scales[:], grouped[:])
             for i in range(first // P, (first + width) // P):
                 cols = slice(i * P - first, (i + 1) * P - first)

@@ -41,13 +41,16 @@ def tile_list_engram_dl_add_kernel(
         psum = ctx.enter_context(tc.psum_pool(name="psum", bufs=1))
 
         offsets = keep.tile([P, J // LIST_ROWS], U16, name="offsets", align_bytes=256)
-        tab_sc = keep.tile([P, PASSES, T], U8, name="tab_sc", align_bytes=256)
+        tab_sc = keep.tile([P, T], U8, name="tab_sc", align_bytes=256)
+        picked_sc = keep.tile([P, J], U8, name="picked_sc", align_bytes=256)
+        moved_sc = keep.tile([P, J], U8, name="moved_sc", align_bytes=256)
         wk_sc = keep.tile([P, PASSES, N], U8, name="wk_sc", align_bytes=256)
         wv_sc = keep.tile([P, PASSES, N], U8, name="wv_sc", align_bytes=256)
         tab_w = keep.tile([P, T], I32, name="tab_w", align_bytes=256)
 
         nc.vector.memset(tab_sc[:].bitcast(I32), 0)
         nc.vector.memset(wk_sc[:].bitcast(I32), 0)
+        nc.vector.memset(moved_sc[:].bitcast(I32), 0)
         nc.gpsimd.memset(wv_sc[:].bitcast(I32), 0)
 
         wvd_raw, st_sb, res_sb = {}, {}, {}
@@ -83,14 +86,19 @@ def tile_list_engram_dl_add_kernel(
         table = tab_words[0].rearrange("p t b -> p (t b)").bitcast(I32)
         nc.sync.dma_start(tab_w[:, : T // 2], table[:, : T // 2])
         nc.sync.dma_start(offsets[:], offs)
-        load_scales(nc.sync, tab_sc, tab_scales)
+        tab_rows = tab_scales.rearrange("a (q r) n -> r q a n", r=4)
+        for r in range(4):
+            nc.sync.dma_start(tab_sc[r:P:16, :].bitcast(I32), tab_rows[r].bitcast(I32))
         nc.sync.dma_start(tab_w[:, T // 2 :], table[:, T // 2 :])
         wk_w = load_words("wk_w", wk_words)
         load_scales(nc.sync, wk_sc, wk_scales)
         wv_w = load_words("wv_w", wv4_words)
         load_wvd(0, 0, N // 2)
-        load_scales(nc.sync, wv_sc, wv4_scales)
+        nc.vector.tensor_copy(picked_sc[:], tab_sc[:].indirect(offsets[:]))
+        for r in range(4):
+            nc.sync.dma_start(moved_sc[r:P:32, :].bitcast(I32), picked_sc[16 + r : P : 32, :].bitcast(I32))
         load_wvd(1, 0, N // 2)
+        load_scales(nc.sync, wv_sc, wv4_scales)
         load_rows("st", st, st_sb, 0, 2)
         load_rows("st", st, st_sb, 2, 2)
         load_wvd(0, N // 2, N)
@@ -107,9 +115,9 @@ def tile_list_engram_dl_add_kernel(
         def picks(h):
             return offsets[:, h * (HALF // LIST_ROWS) : (h + 1) * (HALF // LIST_ROWS)]
 
-        def gather_scales(h, a, planes):
-            v_sc[h, a] = planes
-            nc.vector.tensor_copy(v_sc[h, a], tab_sc[:, a, :].indirect(picks(h)))
+        for h in range(2):
+            for a, plane in enumerate((picked_sc, moved_sc)):
+                v_sc[h, a] = plane[:, h * HALF : (h + 1) * HALF]
 
         def gather_words(h, both):
             nc.vector.tensor_copy(both.bitcast(U32), tab_w[:].bitcast(U32).indirect(picks(h)))
@@ -122,23 +130,16 @@ def tile_list_engram_dl_add_kernel(
 
         def gather_first_pass():
             both = keep.tile([P, 4 * HALF], U8, name="picked0", tag="picked", align_bytes=256)
-            plane = keep.tile([P, HALF], U8, name="plane00", align_bytes=256)
             parted, paired = by_pass(0, both[:])
-            gather_scales(0, 0, plane[:])
             gather_words(0, both[:])
             for a in range(PASSES):
                 nc.vector.tensor_copy(parted[:, a, :], paired[:, a, :])
 
         def gather_rest():
-            picked = keep.tile([P, 6 * HALF], U8, name="picked1", tag="picked", align_bytes=256)
-            both = picked[:, : 4 * HALF]
-            parted, paired = by_pass(1, both)
-            gather_scales(0, 1, picked[:, 5 * HALF :])
-            gather_words(1, both)
-            gather_scales(1, 0, picked[:, 4 * HALF : 5 * HALF])
+            both = keep.tile([P, 4 * HALF], U8, name="picked1", tag="picked", align_bytes=256)
+            parted, paired = by_pass(1, both[:])
+            gather_words(1, both[:])
             nc.vector.tensor_copy(parted, paired)
-            last = keep.tile([P, HALF], U8, name="last_plane", tag="stage00", align_bytes=256)
-            gather_scales(1, 1, last[:])
 
         wd_codes, wd_sc = {}, {}
 
@@ -200,7 +201,12 @@ def tile_list_engram_dl_add_kernel(
         def value(i, h, number):
             gate = st_sb[i][:, h * HALF : (h + 1) * HALF]
             ve = bank(number)
-            if i <= EARLY:
+            if i < EARLY and h == 0:
+                fp8_pass(ve, i, h, 0, True, False)
+                for a in range(PASSES):
+                    fp4_pass(ve, wv_w, wv_sc, i, h, a, False, False)
+                fp8_pass(ve, i, h, 1, False, True)
+            elif i <= EARLY:
                 for a in range(PASSES):
                     fp4_pass(ve, wv_w, wv_sc, i, h, a, a == 0, False)
                 for a in range(PASSES):

@@ -28,6 +28,7 @@ LIST_ROWS = 16
 KEY_BANKS, VALUE_BANKS = 4, 4
 PIECES = tuple((c, c + GROUP) for c in range(0, N, GROUP))
 VECTOR_ADDS = ((ROW_TILES - 2, 1), (ROW_TILES - 1, 0), (ROW_TILES - 1, 1))
+WHOLE_ADDS = (3, 4, 5)
 EARLY = 4
 KEYS_AHEAD = 2
 
@@ -206,7 +207,7 @@ def tile_list_engram_dl_add_kernel(
                 for a in range(PASSES):
                     fp4_pass(ve, wv_w, wv_sc, i, h, a, False, False)
                 fp8_pass(ve, i, h, 1, False, True)
-            elif i <= EARLY:
+            elif i <= EARLY + 1:
                 for a in range(PASSES):
                     fp4_pass(ve, wv_w, wv_sc, i, h, a, a == 0, False)
                 for a in range(PASSES):
@@ -221,7 +222,10 @@ def tile_list_engram_dl_add_kernel(
         def finish(i, h):
             cols = slice(h * HALF, (h + 1) * HALF)
             adder = nc.vector if (i, h) in VECTOR_ADDS else nc.gpsimd
-            adder.tensor_tensor(res_sb[i][:, cols], res_sb[i][:, cols], st_sb[i][:, cols], ADD)
+            if i not in WHOLE_ADDS:
+                adder.tensor_tensor(res_sb[i][:, cols], res_sb[i][:, cols], st_sb[i][:, cols], ADD)
+            elif h == 1:
+                adder.tensor_tensor(res_sb[i], res_sb[i], st_sb[i], ADD)
             if i == ROW_TILES - 1:
                 nc.sync.dma_start(out[i * P : (i + 1) * P, cols], res_sb[i][:, cols])
             elif h == 1 and i >= EARLY:

@@ -184,6 +184,10 @@ def tile_list_engram_dl_add_kernel(
         def bank(number):
             return psum.tile([P, HALF], F32, name="bank%d" % number, bufs=1)
 
+        def pieces_of(i, h):
+            width = HALF // 2 if (i, h) == (ROW_TILES - 1, 1) else HALF
+            return [slice(c, c + width) for c in range(0, HALF, width)]
+
         opened = {}
 
         def open_key(i, h, number):
@@ -217,18 +221,23 @@ def tile_list_engram_dl_add_kernel(
                     fp8_pass(ve, i, h, a, a == PASSES - 1, False)
                 for a in range(PASSES):
                     fp4_pass(ve, wv_w, wv_sc, i, h, a, False, a == PASSES - 1)
-            nc.vector.tensor_tensor(gate, gate, ve[:], MULT)
+            for cols in pieces_of(i, h):
+                nc.vector.tensor_tensor(gate[:, cols], gate[:, cols], ve[:, cols], MULT)
 
         def finish(i, h):
             cols = slice(h * HALF, (h + 1) * HALF)
             adder = nc.vector if (i, h) in VECTOR_ADDS else nc.gpsimd
+            if i == ROW_TILES - 1:
+                for piece in pieces_of(i, h):
+                    total = res_sb[i][:, cols][:, piece]
+                    adder.tensor_tensor(total, total, st_sb[i][:, cols][:, piece], ADD)
+                nc.sync.dma_start(out[i * P : (i + 1) * P, cols], res_sb[i][:, cols])
+                return
             if i not in WHOLE_ADDS:
                 adder.tensor_tensor(res_sb[i][:, cols], res_sb[i][:, cols], st_sb[i][:, cols], ADD)
             elif h == 1:
                 adder.tensor_tensor(res_sb[i], res_sb[i], st_sb[i], ADD)
-            if i == ROW_TILES - 1:
-                nc.sync.dma_start(out[i * P : (i + 1) * P, cols], res_sb[i][:, cols])
-            elif h == 1 and i >= EARLY:
+            if h == 1 and i >= EARLY:
                 nc.sync.dma_start(out[i * P : (i + 1) * P, :], res_sb[i])
             elif h == 1 and i % 2 == 1:
                 nc.sync.dma_start(rows_of(out, i - 1, 2), res_pair[i - 1][:])

from contextlib import ExitStack

import concourse.mybir as mybir

K, N, T, J = 1024, 1024, 2048, 1024
FLOPS = 3 * 2 * K * N * J

F32 = mybir.dt.float32
BF16 = mybir.dt.bfloat16
I32 = mybir.dt.int32
U32 = mybir.dt.uint32
U16 = mybir.dt.uint16
U8 = mybir.dt.uint8
FP8X4 = mybir.dt.float8_e4m3fn_x4
FP4X4 = mybir.dt.float4_e2m1fn_x4
ADD = mybir.AluOpType.add
MULT = mybir.AluOpType.mult
SIGMOID = mybir.ActivationFunctionType.Sigmoid

P = 128
PACK = 4
K_PASS = P * PACK
PASSES = K // K_PASS
HALF = 512
GROUP = 256
ROW_TILES = N // P
LIST_ROWS = 16
KEY_BANKS, VALUE_BANKS = 4, 4
PIECES = tuple((c, c + GROUP) for c in range(0, N, GROUP))
VECTOR_ADDS = ((ROW_TILES - 2, 1), (ROW_TILES - 1, 0), (ROW_TILES - 1, 1))
WHOLE_ADDS = (3, 4, 5)
EARLY = 4
KEYS_AHEAD = 2


def tile_list_engram_dl_add_kernel(
    tc, tab_words, tab_scales, wk_words, wk_scales, wv4_words, wv4_scales, wvd, st, res, offs, out
):
    nc = tc.nc
    with ExitStack() as ctx:
        keep = ctx.enter_context(tc.tile_pool(name="keep", bufs=1))
        psum = ctx.enter_context(tc.psum_pool(name="psum", bufs=1))

        offsets = keep.tile([P, J // LIST_ROWS], U16, name="offsets", align_bytes=256)
        tab_sc = keep.tile([P, T], U8, name="tab_sc", align_bytes=256)
        picked_sc = keep.tile([P, J], U8, name="picked_sc", align_bytes=256)
        moved_sc = keep.tile([P, J], U8, name="moved_sc", align_bytes=256)
        wk_sc = keep.tile([P, PASSES, N], U8, name="wk_sc", align_bytes=256)
        wv_sc = keep.tile([P, PASSES, N], U8, name="wv_sc", align_bytes=256)
        tab_w = keep.tile([P, T], I32, name="tab_w", align_bytes=256)

        nc.vector.memset(tab_sc[:].bitcast(I32), 0)
        nc.vector.memset(wk_sc[:].bitcast(I32), 0)
        nc.vector.memset(moved_sc[:].bitcast(I32), 0)
        nc.gpsimd.memset(wv_sc[:].bitcast(I32), 0)

        wvd_raw, st_sb, res_sb = {}, {}, {}

        def load_scales(queue, plane, dram):
            rows = dram.rearrange("a (q r) n -> r q a n", r=4)
            for r in range(4):
                queue.dma_start(plane[r:P:32, :, :].bitcast(I32), rows[r].bitcast(I32))

        def load_words(name, dram):
            words = keep.tile([P, PASSES, 2 * N], U8, name=name, align_bytes=256)
            nc.sync.dma_start(words[:].bitcast(I32), dram.rearrange("a p b -> p a b").bitcast(I32))
            return words

        def load_wvd(a, c0, c1):
            raw = keep.tile([P, PACK, c1 - c0], F32, name="wvd_raw_%d_%d" % (a, c0), align_bytes=256)
            src = wvd[K_PASS * a : K_PASS * (a + 1), c0:c1].rearrange("(p t) n -> p t n", t=PACK)
            nc.sync.dma_start(raw[:], src)
            for first, last in PIECES:
                if c0 <= first and last <= c1:
                    wvd_raw[a, first] = raw[:, :, first - c0 : last - c0]

        def rows_of(dram, first, count):
            return dram[P * first : P * (first + count), :].rearrange("(i p) j -> p i j", p=P)

        def load_rows(name, dram, tiles, first, count):
            held = keep.tile([P, count, J], F32, name="%s_%d" % (name, first), align_bytes=256)
            nc.sync.dma_start(held[:], rows_of(dram, first, count))
            for i in range(count):
                tiles[first + i] = held[:, i, :]
            return held

        table = tab_words[0].rearrange("p t b -> p (t b)").bitcast(I32)
        nc.sync.dma_start(tab_w[:, : T // 2], table[:, : T // 2])
        nc.sync.dma_start(offsets[:], offs)
        tab_rows = tab_scales.rearrange("a (q r) n -> r q a n", r=4)
        for r in range(4):
            nc.sync.dma_start(tab_sc[r:P:16, :].bitcast(I32), tab_rows[r].bitcast(I32))
        nc.sync.dma_start(tab_w[:, T // 2 :], table[:, T // 2 :])
        wk_w = load_words("wk_w", wk_words)
        load_scales(nc.sync, wk_sc, wk_scales)
        wv_w = load_words("wv_w", wv4_words)
        load_wvd(0, 0, N // 2)
        nc.vector.tensor_copy(picked_sc[:], tab_sc[:].indirect(offsets[:]))
        for r in range(4):
            nc.sync.dma_start(moved_sc[r:P:32, :].bitcast(I32), picked_sc[16 + r : P : 32, :].bitcast(I32))
        load_wvd(1, 0, N // 2)
        load_scales(nc.sync, wv_sc, wv4_scales)
        load_rows("st", st, st_sb, 0, 2)
        load_rows("st", st, st_sb, 2, 2)
        load_wvd(0, N // 2, N)
        res_pair = {0: load_rows("res", res, res_sb, 0, 2)}
        load_wvd(1, N // 2, N)
        res_pair[2] = load_rows("res", res, res_sb, 2, 2)
        load_rows("st", st, st_sb, 4, 2)
        load_rows("res", res, res_sb, 4, 2)
        load_rows("st", st, st_sb, 6, 2)
        load_rows("res", res, res_sb, 6, 2)

        v_w, v_sc = {}, {}

        def picks(h):
            return offsets[:, h * (HALF // LIST_ROWS) : (h + 1) * (HALF // LIST_ROWS)]

        for h in range(2):
            for a, plane in enumerate((picked_sc, moved_sc)):
                v_sc[h, a] = plane[:, h * HALF : (h + 1) * HALF]

        def gather_words(h, both):
            nc.vector.tensor_copy(both.bitcast(U32), tab_w[:].bitcast(U32).indirect(picks(h)))

        def by_pass(h, both):
            parted = keep.tile([P, PASSES, 2 * HALF], U8, name="v_w_%d" % h, align_bytes=256)
            for a in range(PASSES):
                v_w[h, a] = parted[:, a, :]
            return parted[:].bitcast(U16), both.bitcast(U16).rearrange("p (j d) -> p d j", d=PASSES)

        def gather_first_pass():
            both = keep.tile([P, 4 * HALF], U8, name="picked0", tag="picked", align_bytes=256)
            parted, paired = by_pass(0, both[:])
            gather_words(0, both[:])
            for a in range(PASSES):
                nc.vector.tensor_copy(parted[:, a, :], paired[:, a, :])

        def gather_rest():
            both = keep.tile([P, 4 * HALF], U8, name="picked1", tag="picked", align_bytes=256)
            parted, paired = by_pass(1, both[:])
            gather_words(1, both[:])
            nc.vector.tensor_copy(parted, paired)

        wd_codes, wd_sc = {}, {}

        def quantise(groups, a, stage, copy):
            first, width = PIECES[groups[0]][0], GROUP * len(groups)
            grouped = keep.tile([P, width * PACK], BF16, name="grouped_%d_%d" % (first, a), tag=stage, align_bytes=256)
            for place, g in enumerate(groups):
                copy(
                    grouped[:, place * GROUP * PACK : (place + 1) * GROUP * PACK].rearrange("p (c i t) -> p c t i", i=4, t=PACK),
                    wvd_raw[a, PIECES[g][0]].rearrange("p t (c i) -> p c t i", i=4),
                )
            codes = keep.tile([P, width], U32, name="wd_codes_%d_%d" % (first, a), align_bytes=256)
            scales = keep.tile([P, width], U8, name="wd_sc_%d_%d" % (first, a), align_bytes=256)
            nc.vector.quantize_mx(codes[:].bitcast(FP8X4), scales[:], grouped[:])
            for i in range(first // P, (first + width) // P):
                cols = slice(i * P - first, (i + 1) * P - first)
                wd_codes[i, a], wd_sc[i, a] = codes[:, cols], scales[:, cols]

        def fp4_pass(acc, words, plane, i, h, a, start, stop):
            nc.tensor.matmul_mx(
                acc[:],
                lhsT=words[:, a, 2 * i * P : 2 * (i + 1) * P].bitcast(FP4X4),
                lhsT_scale=plane[:, a, i * P : (i + 1) * P],
                rhs=v_w[h, a].bitcast(FP4X4),
                rhs_scale=v_sc[h, a],
                start=start,
                stop=stop,
            )

        def fp8_pass(acc, i, h, a, start, stop):
            nc.tensor.matmul_mx(
                acc[:],
                lhsT=wd_codes[i, a].bitcast(FP8X4),
                lhsT_scale=wd_sc[i, a],
                rhs=v_w[h, a].bitcast(FP4X4),
                rhs_scale=v_sc[h, a],
                start=start,
                stop=stop,
            )

        def bank(number):
            return psum.tile([P, HALF], F32, name="bank%d" % number, bufs=1)

        def pieces_of(i, h):
            width = HALF // 2 if (i, h) == (ROW_TILES - 1, 1) else HALF
            return [slice(c, c + width) for c in range(0, HALF, width)]

        opened = {}

        def open_key(i, h, number):
            opened[i, h] = bank(number)
            fp4_pass(opened[i, h], wk_w, wk_sc, i, h, 0, True, False)

        def key(i, h, number):
            gate = st_sb[i][:, h * HALF : (h + 1) * HALF]
            if (i, h) not in opened:
                open_key(i, h, number)
            ke = opened[i, h]
            fp4_pass(ke, wk_w, wk_sc, i, h, 1, False, True)
            nc.vector.tensor_tensor(gate, gate, ke[:], ADD)
            nc.scalar.activation(gate, gate, SIGMOID)

        def value(i, h, number):
            gate = st_sb[i][:, h * HALF : (h + 1) * HALF]
            ve = bank(number)
            if i < EARLY and h == 0:
                fp8_pass(ve, i, h, 0, True, False)
                for a in range(PASSES):
                    fp4_pass(ve, wv_w, wv_sc, i, h, a, False, False)
                fp8_pass(ve, i, h, 1, False, True)
            elif i <= EARLY + 1:
                for a in range(PASSES):
                    fp4_pass(ve, wv_w, wv_sc, i, h, a, a == 0, False)
                for a in range(PASSES):
                    fp8_pass(ve, i, h, a, False, a == PASSES - 1)
            else:
                for a in reversed(range(PASSES)):
                    fp8_pass(ve, i, h, a, a == PASSES - 1, False)
                for a in range(PASSES):
                    fp4_pass(ve, wv_w, wv_sc, i, h, a, False, a == PASSES - 1)
            for cols in pieces_of(i, h):
                nc.vector.tensor_tensor(gate[:, cols], gate[:, cols], ve[:, cols], MULT)

        def finish(i, h):
            cols = slice(h * HALF, (h + 1) * HALF)
            adder = nc.vector if (i, h) in VECTOR_ADDS else nc.gpsimd
            if i == ROW_TILES - 1:
                for piece in pieces_of(i, h):
                    total = res_sb[i][:, cols][:, piece]
                    adder.tensor_tensor(total, total, st_sb[i][:, cols][:, piece], ADD)
                nc.sync.dma_start(out[i * P : (i + 1) * P, cols], res_sb[i][:, cols])
                return
            if i not in WHOLE_ADDS:
                adder.tensor_tensor(res_sb[i][:, cols], res_sb[i][:, cols], st_sb[i][:, cols], ADD)
            elif h == 1:
                adder.tensor_tensor(res_sb[i], res_sb[i], st_sb[i], ADD)
            if h == 1 and i >= EARLY:
                nc.sync.dma_start(out[i * P : (i + 1) * P, :], res_sb[i])
            elif h == 1 and i % 2 == 1:
                nc.sync.dma_start(rows_of(out, i - 1, 2), res_pair[i - 1][:])

        units = [(i, h) for h in range(2) for i in range(4)] + [(i, h) for i in range(4, ROW_TILES) for h in range(2)]
        banks = [(0, 4), (1, 5), (2, 6), (3, 7)] + [(1, 0), (4, 5), (2, 6), (3, 7)] * 3
        gather_first_pass()
        for u in range(EARLY):
            open_key(*units[u], banks[u][0])
        quantise([0], 0, "stage00", nc.scalar.copy)
        gather_rest()
        for u in range(KEYS_AHEAD):
            key(*units[u], banks[u][0])
        for g, a in ((0, 1), (1, 0), (1, 1)):
            quantise([g], a, "stage%d%d" % (g, a), nc.scalar.copy)
        for u, (i, h) in enumerate(units):
            if u == EARLY:
                quantise([2, 3], 0, "stage20", nc.scalar.copy)
                quantise([2, 3], 1, "stage21", nc.scalar.copy)
            if u + KEYS_AHEAD < len(units):
                key(*units[u + KEYS_AHEAD], banks[u + KEYS_AHEAD][0])
            value(i, h, banks[u][1])
            finish(i, h)
